import numpy as np
import ml_dtypes


def mxq(x, axis, fmt="e4m3"):
    dtype, down = {"e4m3": (ml_dtypes.float8_e4m3fn, 7), "e5m2": (ml_dtypes.float8_e5m2, 14)}[fmt]
    v = np.moveaxis(np.asarray(x, np.float32).astype(ml_dtypes.bfloat16).astype(np.float64), axis, -1)
    blocks = v.reshape(v.shape[:-1] + (-1, 32))
    amax = np.abs(blocks).max(-1, keepdims=True)
    byte = np.maximum(np.where(amax > 0, np.frexp(amax)[1] - 1 + 127, 0) - down, 1)
    scale = np.exp2(byte - 127.0)
    codes = (blocks / scale).astype(np.float32).astype(dtype).astype(np.float64)
    return np.moveaxis((codes * scale).reshape(v.shape), -1, axis)


WIDE = False


def mx_kscale(k):
    if not WIDE:
        return np.ones(k)
    levels = np.array([10, -10, 5, -5, 0])
    if k % 512:
        return np.exp2(np.random.permutation(np.resize(levels, k // 32))).repeat(32)
    a = np.empty((k // 512, 16))
    for p in range(k // 512):
        a[p, :8] = np.random.permutation(np.resize(levels, 8))
        for g in range(8):
            far = levels[np.abs(levels - a[p, g]) >= 10]
            a[p, g + 8] = far[np.random.randint(len(far))]
    return np.exp2(a.ravel()).repeat(32)


def f64(x):
    return np.asarray(x).astype(np.float64)


def striped(idx):
    return np.tile(idx.reshape(-1, 16).T, (8, 1)).astype(np.uint16)


def unstriped(offs):
    return offs[:16].T.reshape(-1).astype(np.int64)


def relu(v):
    return np.maximum(v, 0.0)

def planes(y):
    n, m = y.shape
    v = y.astype(np.float32).astype(ml_dtypes.bfloat16).astype(np.float64).reshape(n // 32, 32, m)
    top = np.abs(v).max(1)
    byte = np.clip(np.where(top > 0, np.frexp(top)[1] - 1 + 127 - 7, 1), 1, 254)
    codes = (v * np.exp2(127.0 - byte)[:, None, :]).reshape(n, m).astype(np.float32).astype(ml_dtypes.float8_e4m3fn).view(np.uint8)
    words = codes.reshape(n // 512, 128, 4, m).transpose(0, 1, 3, 2)
    return np.ascontiguousarray(words), np.ascontiguousarray(byte.astype(np.uint8).reshape(n // 512, 16, m))


K, T, S, N, U = 512, 2048, 1024, 512, 2048


def setup_inputs():
    n = np.random.standard_normal
    s = mx_kscale(K)[:, None]
    return {
        "xT": (n((K, T)) * s).astype(np.float32),
        "w1": (n((K, N)) / np.sqrt(K) / s).astype(np.float32),
        "res": n((N, U)).astype(np.float32),
        "offs": striped(np.random.permutation(T)[:S]),
        "own": striped(np.random.randint(0, S, U)),
    }


def reference(xT, w1, res, offs, own):
    xq = mxq(f64(xT)[:, unstriped(offs)], 0, "e4m3")
    y = relu(mxq(f64(w1), 0, "e4m3").T @ xq)
    out_0 = f64(res) + y[:, unstriped(own)]
    return (out_0,) + planes(out_0)

@@ -1,0 +1,185 @@
+from contextlib import ExitStack
+
+import concourse.mybir as mybir
+
+K, T, S, N, U = 512, 2048, 1024, 512, 2048
+FLOPS = 2 * K * N * S
+
+F32 = mybir.dt.float32
+BF16 = mybir.dt.bfloat16
+U32 = mybir.dt.uint32
+I32 = mybir.dt.int32
+U16 = mybir.dt.uint16
+U8 = mybir.dt.uint8
+FP8X4 = mybir.dt.float8_e4m3fn_x4
+RELU = mybir.ActivationFunctionType.Relu
+ADD = mybir.AluOpType.add
+
+P = 128
+PACK = 4
+LIST = 16
+LINE = 4
+
+X_LOADS = (((0, 1024), (1024, 2048)), ((0, 1024), (1024, 1536), (1536, 2048)))
+PICKED = ((0, 512), (512, 768), (768, 1024))
+W_LOADS = ((0, 256), (256, 512))
+HEAD = 1024
+TAIL = ((1024, 1536), (1536, 1792), (1792, 1920), (1920, 2048))
+
+
+def tile_picked_unmerge_relu_lo_kernel(tc, xT, w1, res, offs, own, out_0, out_1, out_2):
+    nc = tc.nc
+    x_rows = xT.rearrange("(p j) c -> p j c", j=PACK)
+    w_rows = w1.rearrange("(p j) c -> p j c", j=PACK)
+    res_rows = res.rearrange("(p j) c -> p j c", j=PACK)
+    out_rows = out_0.rearrange("(p j) c -> p j c", j=PACK)
+    out_words = out_1[0].rearrange("p c r -> p (c r)").bitcast(I32)
+    out_scales = out_2[0].bitcast(I32)
+
+    with ExitStack() as ctx:
+        lists = ctx.enter_context(tc.tile_pool(name="lists", bufs=1))
+        keep = ctx.enter_context(tc.tile_pool(name="keep", bufs=1))
+        psum = ctx.enter_context(tc.psum_pool(name="psum", bufs=8))
+
+        offs_sb = lists.tile([P, S // LIST], U16, name="offs_sb")
+        own_sb = lists.tile([P, U // LIST], U16, name="own_sb")
+
+        x_raw = {}
+        for h in range(2):
+            for a, b in X_LOADS[h]:
+                x_raw[h, a] = keep.tile([P, 2, b - a], F32, name="x_raw_%d_%d" % (h, a))
+                nc.sync.dma_start(x_raw[h, a][:], x_rows[:, 2 * h : 2 * h + 2, a:b])
+                if (h, a) == (0, 0):
+                    nc.sync.dma_start(offs_sb[:], offs)
+        w_raw = {}
+        for a, b in W_LOADS:
+            w_raw[a] = keep.tile([P, PACK, b - a], F32, name="w_raw_%d" % a)
+            nc.sync.dma_start(w_raw[a][:], w_rows[:, :, a:b])
+        nc.sync.dma_start(own_sb[:], own)
+        res_head = []
+        for t in range(PACK):
+            res_head.append(keep.tile([P, HEAD], F32, name="res_head_%d" % t))
+            nc.sync.dma_start(res_head[t][:], res_rows[:, t, 0:HEAD])
+        res_tail = {}
+        for a in (1024, 1536):
+            res_tail[a] = keep.tile([P, PACK, 512], F32, name="res_tail_%d" % a)
+            nc.sync.dma_start(res_tail[a][:], res_rows[:, :, a : a + 512])
+
+        pairs = [keep.tile([P, T * 2], BF16, name="pairs_%d" % h) for h in range(2)]
+
+        def cast_pairs(engine, h, load, a, b):
+            src = x_raw[h, load][:, :, a - load : b - load].rearrange("p e (c i) -> p c e i", i=LINE)
+            dst = pairs[h][:, 2 * a : 2 * b].rearrange("p (c i e) -> p c e i", i=LINE, e=2)
+            if engine == "scalar":
+                nc.scalar.copy(dst, src)
+            else:
+                nc.vector.tensor_copy(dst, src)
+
+        picked = [keep.tile([P, (b - a) * PACK], BF16, name="picked_%d" % a, align_bytes=64) for a, b in PICKED]
+
+        def gather_pairs(h, n):
+            a, b = PICKED[n]
+            dst = picked[n][:].bitcast(U32).rearrange("p (s h) -> p s h", h=2)[:, :, h]
+            nc.vector.tensor_copy(dst, pairs[h][:].bitcast(U32).indirect(offs_sb[:, a // LIST : b // LIST]))
+
+        cast_pairs("scalar", 0, 0, 0, 1024)
+        cast_pairs("vector", 0, 1024, 1024, 1728)
+        cast_pairs("scalar", 0, 1024, 1728, 2048)
+        for n in range(3):
+            gather_pairs(0, n)
+        cast_pairs("scalar", 1, 0, 0, 1024)
+        cast_pairs("vector", 1, 1024, 1024, 1536)
+        cast_pairs("vector", 1, 1536, 1536, 2048)
+
+        w_first = keep.tile([P, P * PACK], BF16, name="w_first", tag="shared", align_bytes=64)
+        w_rest = keep.tile([P, 3 * P * PACK], BF16, name="w_rest", align_bytes=64)
+        w_codes = keep.tile([P, N], U32, name="w_codes", align_bytes=64)
+        w_scales = keep.tile([P, N], U8, name="w_scales", align_bytes=64)
+        for a, b in W_LOADS:
+            src = w_raw[a][:].rearrange("p j (m t) -> p m j t", t=PACK)
+            m0, m1 = a // PACK, b // PACK
+            nc.scalar.copy(w_first[:].rearrange("p (m j) -> p m j", j=PACK)[:, m0:m1, :], src[:, :, :, 0])
+            nc.scalar.copy(w_rest[:].rearrange("p (t m j) -> p m j t", t=3, j=PACK)[:, m0:m1, :, :], src[:, :, :, 1:PACK])
+
+        x_codes = [None, None, None]
+        x_scales = [keep.tile([P, b - a], U8, name="x_scales_%d" % a, align_bytes=64) for a, b in PICKED]
+
+        def quantize_x(n, tag):
+            a, b = PICKED[n]
+            x_codes[n] = keep.tile([P, b - a], U32, name="x_codes_%d" % a, tag=tag, align_bytes=64)
+            nc.vector.quantize_mx(out=x_codes[n][:].bitcast(FP8X4), scales=x_scales[n][:], in_=picked[n][:])
+
+        gather_pairs(1, 0)
+        gather_pairs(1, 1)
+        quantize_x(0, "x_codes_0")
+        gather_pairs(1, 2)
+        nc.vector.quantize_mx(out=w_codes[:, 0:P].bitcast(FP8X4), scales=w_scales[:, 0:P], in_=w_first[:])
+        quantize_x(1, "shared")
+        quantize_x(2, "x_codes_2")
+        nc.vector.quantize_mx(out=w_codes[:, P : 2 * P].bitcast(FP8X4), scales=w_scales[:, P : 2 * P], in_=w_rest[:, 0 : P * PACK])
+        nc.vector.quantize_mx(out=w_codes[:, 2 * P :].bitcast(FP8X4), scales=w_scales[:, 2 * P :], in_=w_rest[:, P * PACK :])
+
+        y = []
+        for t in range(PACK):
+            y.append(keep.tile([P, S], F32, name="y_%d" % t))
+            groups = ((0,), (1,), (2,)) if t == 0 else ((0,), (1, 2))
+            for group in groups:
+                acc = psum.tile([P, 512], F32, name="acc")
+                first = PICKED[group[0]][0]
+                for n in group:
+                    a, b = PICKED[n]
+                    nc.tensor.matmul_mx(
+                        out=acc[:, a - first : b - first],
+                        lhsT=w_codes[:, t * P : (t + 1) * P].bitcast(FP8X4),
+                        lhsT_scale=w_scales[:, t * P : (t + 1) * P],
+                        rhs=x_codes[n][:].bitcast(FP8X4),
+                        rhs_scale=x_scales[n][:],
+                        start=True,
+                        stop=True,
+                    )
+                last = PICKED[group[-1]][1]
+                nc.scalar.activation(y[t][:, first:last], acc[:, 0 : last - first], RELU)
+
+        scales = keep.tile([P, U], U8, name="scales", align_bytes=64)
+
+        def fetch_add(dst, t, residual, a, b):
+            nc.vector.tensor_tensor(dst, y[t][:].indirect(own_sb[:, a // LIST : b // LIST]), residual, ADD)
+
+        def round_out(engine, summed, a, b):
+            rounded = keep.tile([P, (b - a) * PACK], BF16, name="rounded_%d" % a, align_bytes=64)
+            src = summed.rearrange("p t (c i) -> p c t i", i=LINE)
+            dst = rounded[:].rearrange("p (c i t) -> p c t i", i=LINE, t=PACK)
+            if engine == "scalar":
+                nc.scalar.copy(dst, src)
+            else:
+                nc.vector.tensor_copy(dst, src)
+            return rounded
+
+        def quantize_out(rounded, a, b):
+            words = keep.tile([P, b - a], U32, name="words_%d" % a, align_bytes=64)
+            nc.vector.quantize_mx(out=words[:].bitcast(FP8X4), scales=scales[:, a:b], in_=rounded[:])
+            nc.sync.dma_start(out_words[:, a:b], words[:].bitcast(I32))
+
+        def store_scales(a, b, queues):
+            for q in range(4):
+                queues[q].dma_start(out_scales[4 * q : 4 * q + 4, a // 4 : b // 4], scales[32 * q : 32 * q + 4, a:b].bitcast(I32))
+
+        head = keep.tile([P, PACK, HEAD], F32, name="head")
+        for t in range(PACK):
+            for a in (0, 512):
+                fetch_add(head[:, t, a : a + 512], t, res_head[t][:, a : a + 512], a, a + 512)
+            nc.sync.dma_start(out_rows[:, t, 0:HEAD], head[:, t, :])
+        waiting = [(round_out("scalar", head[:, :, a : a + 512], a, a + 512), a, a + 512) for a in (0, 512)]
+        for a, b in TAIL:
+            summed = keep.tile([P, PACK, b - a], F32, name="summed_%d" % a)
+            load = 1024 if a < 1536 else 1536
+            for t in range(PACK):
+                fetch_add(summed[:, t, :], t, res_tail[load][:, t, a - load : b - load], a, b)
+            nc.sync.dma_start(out_rows[:, :, a:b], summed[:])
+            for item in waiting:
+                quantize_out(*item)
+            if a == 1536:
+                store_scales(0, 1536, [nc.sync] * 4)
+            waiting = [(round_out("scalar" if b < U else "vector", summed[:], a, b), a, b)]
+        quantize_out(*waiting[0])
+        store_scales(1536, U, [nc.scalar, nc.scalar, nc.sync, nc.sync])

@@ -20,11 +20,11 @@ PACK = 4
 LIST = 16
 LINE = 4
 
-X_LOADS = (((0, 1024), (1024, 2048)), ((0, 1024), (1024, 1536), (1536, 2048)))
+X_LOADS = ((0, 1024), (1024, 1536), (1536, 2048))
 PICKED = ((0, 512), (512, 768), (768, 1024))
 W_LOADS = ((0, 256), (256, 512))
 HEAD = 1024
-TAIL = ((1024, 1536), (1536, 1792), (1792, 1920), (1920, 2048))
+TAIL = ((1024, 1536), (1536, 1792), (1792, 2048))
 
 
 def tile_picked_unmerge_relu_lo_kernel(tc, xT, w1, res, offs, own, out_0, out_1, out_2):
@@ -46,7 +46,7 @@ def tile_picked_unmerge_relu_lo_kernel(tc, xT, w1, res, offs, own, out_0, out_1,
 
         x_raw = {}
         for h in range(2):
-            for a, b in X_LOADS[h]:
+            for a, b in X_LOADS:
                 x_raw[h, a] = keep.tile([P, 2, b - a], F32, name="x_raw_%d_%d" % (h, a))
                 nc.sync.dma_start(x_raw[h, a][:], x_rows[:, 2 * h : 2 * h + 2, a:b])
                 if (h, a) == (0, 0):
@@ -82,14 +82,14 @@ def tile_picked_unmerge_relu_lo_kernel(tc, xT, w1, res, offs, own, out_0, out_1,
             dst = picked[n][:].bitcast(U32).rearrange("p (s h) -> p s h", h=2)[:, :, h]
             nc.vector.tensor_copy(dst, pairs[h][:].bitcast(U32).indirect(offs_sb[:, a // LIST : b // LIST]))
 
-        cast_pairs("scalar", 0, 0, 0, 1024)
-        cast_pairs("vector", 0, 1024, 1024, 1728)
-        cast_pairs("scalar", 0, 1024, 1728, 2048)
-        for n in range(3):
-            gather_pairs(0, n)
-        cast_pairs("scalar", 1, 0, 0, 1024)
-        cast_pairs("vector", 1, 1024, 1024, 1536)
-        cast_pairs("vector", 1, 1536, 1536, 2048)
+        for h in range(2):
+            cast_pairs("scalar", h, 0, 0, 1024)
+            cast_pairs("vector", h, 1024, 1024, 1536)
+            cast_pairs("vector", h, 1536, 1536, 1888)
+            cast_pairs("scalar", h, 1536, 1888, 2048)
+            if h == 0:
+                for n in range(3):
+                    gather_pairs(0, n)
 
         w_first = keep.tile([P, P * PACK], BF16, name="w_first", tag="shared", align_bytes=64)
         w_rest = keep.tile([P, 3 * P * PACK], BF16, name="w_rest", align_bytes=64)
@@ -101,85 +101,83 @@ def tile_picked_unmerge_relu_lo_kernel(tc, xT, w1, res, offs, own, out_0, out_1,
             nc.scalar.copy(w_first[:].rearrange("p (m j) -> p m j", j=PACK)[:, m0:m1, :], src[:, :, :, 0])
             nc.scalar.copy(w_rest[:].rearrange("p (t m j) -> p m j t", t=3, j=PACK)[:, m0:m1, :, :], src[:, :, :, 1:PACK])
 
-        x_codes = [None, None, None]
-        x_scales = [keep.tile([P, b - a], U8, name="x_scales_%d" % a, align_bytes=64) for a, b in PICKED]
+        x_codes = [None, None]
+        x_scales = [keep.tile([P, 512], U8, name="x_scales_%d" % a, align_bytes=64) for a in (0, 512)]
 
-        def quantize_x(n, tag):
+        def quantize_x(n):
             a, b = PICKED[n]
-            x_codes[n] = keep.tile([P, b - a], U32, name="x_codes_%d" % a, tag=tag, align_bytes=64)
-            nc.vector.quantize_mx(out=x_codes[n][:].bitcast(FP8X4), scales=x_scales[n][:], in_=picked[n][:])
+            cols = slice(a % 512, a % 512 + b - a)
+            nc.vector.quantize_mx(out=x_codes[a // 512][:, cols].bitcast(FP8X4), scales=x_scales[a // 512][:, cols], in_=picked[n][:])
 
+        x_codes[0] = keep.tile([P, 512], U32, name="x_codes_0", align_bytes=64)
         gather_pairs(1, 0)
         gather_pairs(1, 1)
-        quantize_x(0, "x_codes_0")
+        quantize_x(0)
         gather_pairs(1, 2)
         nc.vector.quantize_mx(out=w_codes[:, 0:P].bitcast(FP8X4), scales=w_scales[:, 0:P], in_=w_first[:])
-        quantize_x(1, "shared")
-        quantize_x(2, "x_codes_2")
+        x_codes[1] = keep.tile([P, 512], U32, name="x_codes_1", tag="shared", align_bytes=64)
+        quantize_x(1)
+        quantize_x(2)
         nc.vector.quantize_mx(out=w_codes[:, P : 2 * P].bitcast(FP8X4), scales=w_scales[:, P : 2 * P], in_=w_rest[:, 0 : P * PACK])
         nc.vector.quantize_mx(out=w_codes[:, 2 * P :].bitcast(FP8X4), scales=w_scales[:, 2 * P :], in_=w_rest[:, P * PACK :])
 
         y = []
         for t in range(PACK):
             y.append(keep.tile([P, S], F32, name="y_%d" % t))
-            groups = ((0,), (1,), (2,)) if t == 0 else ((0,), (1, 2))
-            for group in groups:
+            width = 256 if t == 0 else 512
+            for a in range(0, S, width):
+                b = a + width
                 acc = psum.tile([P, 512], F32, name="acc")
-                first = PICKED[group[0]][0]
-                for n in group:
-                    a, b = PICKED[n]
-                    nc.tensor.matmul_mx(
-                        out=acc[:, a - first : b - first],
-                        lhsT=w_codes[:, t * P : (t + 1) * P].bitcast(FP8X4),
-                        lhsT_scale=w_scales[:, t * P : (t + 1) * P],
-                        rhs=x_codes[n][:].bitcast(FP8X4),
-                        rhs_scale=x_scales[n][:],
-                        start=True,
-                        stop=True,
-                    )
-                last = PICKED[group[-1]][1]
-                nc.scalar.activation(y[t][:, first:last], acc[:, 0 : last - first], RELU)
+                cols = slice(a % 512, a % 512 + b - a)
+                nc.tensor.matmul_mx(
+                    out=acc[:, 0 : b - a],
+                    lhsT=w_codes[:, t * P : (t + 1) * P].bitcast(FP8X4),
+                    lhsT_scale=w_scales[:, t * P : (t + 1) * P],
+                    rhs=x_codes[a // 512][:, cols].bitcast(FP8X4),
+                    rhs_scale=x_scales[a // 512][:, cols],
+                    start=True,
+                    stop=True,
+                )
+                nc.scalar.activation(y[t][:, a:b], acc[:, 0 : b - a], RELU)
 
         scales = keep.tile([P, U], U8, name="scales", align_bytes=64)
 
         def fetch_add(dst, t, residual, a, b):
             nc.vector.tensor_tensor(dst, y[t][:].indirect(own_sb[:, a // LIST : b // LIST]), residual, ADD)
 
-        def round_out(engine, summed, a, b):
+        def round_out(summed, a, b):
             rounded = keep.tile([P, (b - a) * PACK], BF16, name="rounded_%d" % a, align_bytes=64)
             src = summed.rearrange("p t (c i) -> p c t i", i=LINE)
-            dst = rounded[:].rearrange("p (c i t) -> p c t i", i=LINE, t=PACK)
-            if engine == "scalar":
-                nc.scalar.copy(dst, src)
-            else:
-                nc.vector.tensor_copy(dst, src)
+            nc.scalar.copy(rounded[:].rearrange("p (c i t) -> p c t i", i=LINE, t=PACK), src)
             return rounded
-
-        def quantize_out(rounded, a, b):
-            words = keep.tile([P, b - a], U32, name="words_%d" % a, align_bytes=64)
-            nc.vector.quantize_mx(out=words[:].bitcast(FP8X4), scales=scales[:, a:b], in_=rounded[:])
-            nc.sync.dma_start(out_words[:, a:b], words[:].bitcast(I32))
 
         def store_scales(a, b, queues):
             for q in range(4):
                 queues[q].dma_start(out_scales[4 * q : 4 * q + 4, a // 4 : b // 4], scales[32 * q : 32 * q + 4, a:b].bitcast(I32))
+
+        words = [keep.tile([P, 512], U32, name="words_%d" % a, align_bytes=64) for a in range(0, U, 512)]
+
+        def quantize_out(rounded, a, b):
+            cols = slice(a % 512, a % 512 + b - a)
+            nc.vector.quantize_mx(out=words[a // 512][:, cols].bitcast(FP8X4), scales=scales[:, a:b], in_=rounded[:])
+            if b % 512 == 0:
+                nc.sync.dma_start(out_words[:, b - 512 : b], words[a // 512][:].bitcast(I32))
 
         head = keep.tile([P, PACK, HEAD], F32, name="head")
         for t in range(PACK):
             for a in (0, 512):
                 fetch_add(head[:, t, a : a + 512], t, res_head[t][:, a : a + 512], a, a + 512)
             nc.sync.dma_start(out_rows[:, t, 0:HEAD], head[:, t, :])
-        waiting = [(round_out("scalar", head[:, :, a : a + 512], a, a + 512), a, a + 512) for a in (0, 512)]
+        quantize_out(round_out(head[:, :, 0:512], 0, 512), 0, 512)
+        waiting = [(round_out(head[:, :, 512:HEAD], 512, HEAD), 512, HEAD)]
         for a, b in TAIL:
             summed = keep.tile([P, PACK, b - a], F32, name="summed_%d" % a)
-            load = 1024 if a < 1536 else 1536
+            load = a - a % 512
             for t in range(PACK):
                 fetch_add(summed[:, t, :], t, res_tail[load][:, t, a - load : b - load], a, b)
-            nc.sync.dma_start(out_rows[:, :, a:b], summed[:])
-            for item in waiting:
-                quantize_out(*item)
-            if a == 1536:
-                store_scales(0, 1536, [nc.sync] * 4)
-            waiting = [(round_out("scalar" if b < U else "vector", summed[:], a, b), a, b)]
-        quantize_out(*waiting[0])
-        store_scales(1536, U, [nc.scalar, nc.scalar, nc.sync, nc.sync])
+                if t % 2 == 1:
+                    nc.sync.dma_start(out_rows[:, t - 1 : t + 1, a:b], summed[:, t - 1 : t + 1, :])
+            waiting.append((round_out(summed[:], a, b), a, b))
+        for item in waiting:
+            quantize_out(*item)
+        store_scales(0, U, [nc.scalar, nc.sync, nc.scalar, nc.sync])

@@ -23,8 +23,12 @@ LINE = 4
 X_LOADS = ((0, 1024), (1024, 1536), (1536, 2048))
 PICKED = ((0, 512), (512, 768), (768, 1024))
 W_LOADS = ((0, 256), (256, 512))
-HEAD = 1024
-TAIL = ((1024, 1536), (1536, 1792), (1792, 2048))
+RES_LOADS = ((0, 512), (512, 768), (768, 1664), (1664, 2048))
+CHUNKS = ((0, 512), (512, 768), (768, 1280), (1280, 1664), (1664, 1920), (1920, 2048))
+ROUNDS = ((0, 512), (512, 768), (768, 1024), (1024, 1280), (1280, 1664), (1664, 1920), (1920, 2048))
+QUANTIZE = ((0, 1024), (1024, 1536), (1536, 1664), (1664, 1920), (1920, 2048))
+WORD_STORES = ((0, 1024), (1024, 1536), (1536, 1920), (1920, 2048))
+SCALE_STORES = ((0, 1024), (1024, 2048))
 
 
 def tile_picked_unmerge_relu_lo_kernel(tc, xT, w1, res, offs, own, out_0, out_1, out_2):
@@ -56,14 +60,10 @@ def tile_picked_unmerge_relu_lo_kernel(tc, xT, w1, res, offs, own, out_0, out_1,
             w_raw[a] = keep.tile([P, PACK, b - a], F32, name="w_raw_%d" % a)
             nc.sync.dma_start(w_raw[a][:], w_rows[:, :, a:b])
         nc.sync.dma_start(own_sb[:], own)
-        res_head = []
-        for t in range(PACK):
-            res_head.append(keep.tile([P, HEAD], F32, name="res_head_%d" % t))
-            nc.sync.dma_start(res_head[t][:], res_rows[:, t, 0:HEAD])
-        res_tail = {}
-        for a in (1024, 1536):
-            res_tail[a] = keep.tile([P, PACK, 512], F32, name="res_tail_%d" % a)
-            nc.sync.dma_start(res_tail[a][:], res_rows[:, :, a : a + 512])
+        res_raw = {}
+        for a, b in RES_LOADS:
+            res_raw[a] = keep.tile([P, PACK, b - a], F32, name="res_raw_%d" % a)
+            nc.sync.dma_start(res_raw[a][:], res_rows[:, :, a:b])
 
         pairs = [keep.tile([P, T * 2], BF16, name="pairs_%d" % h) for h in range(2)]
 
@@ -145,39 +145,37 @@ def tile_picked_unmerge_relu_lo_kernel(tc, xT, w1, res, offs, own, out_0, out_1,
         def fetch_add(dst, t, residual, a, b):
             nc.vector.tensor_tensor(dst, y[t][:].indirect(own_sb[:, a // LIST : b // LIST]), residual, ADD)
 
+        rounded = keep.tile([P, U * PACK], BF16, name="rounded", align_bytes=64)
+
         def round_out(summed, a, b):
-            rounded = keep.tile([P, (b - a) * PACK], BF16, name="rounded_%d" % a, align_bytes=64)
             src = summed.rearrange("p t (c i) -> p c t i", i=LINE)
-            nc.scalar.copy(rounded[:].rearrange("p (c i t) -> p c t i", i=LINE, t=PACK), src)
-            return rounded
+            nc.scalar.copy(rounded[:, a * PACK : b * PACK].rearrange("p (c i t) -> p c t i", i=LINE, t=PACK), src)
 
         def store_scales(a, b, queues):
             for q in range(4):
                 queues[q].dma_start(out_scales[4 * q : 4 * q + 4, a // 4 : b // 4], scales[32 * q : 32 * q + 4, a:b].bitcast(I32))
 
-        words = [keep.tile([P, 512], U32, name="words_%d" % a, align_bytes=64) for a in range(0, U, 512)]
+        words = keep.tile([P, U], U32, name="words", align_bytes=64)
 
-        def quantize_out(rounded, a, b):
-            cols = slice(a % 512, a % 512 + b - a)
-            nc.vector.quantize_mx(out=words[a // 512][:, cols].bitcast(FP8X4), scales=scales[:, a:b], in_=rounded[:])
-            if b % 512 == 0:
-                nc.sync.dma_start(out_words[:, b - 512 : b], words[a // 512][:].bitcast(I32))
+        def quantize_out(a, b):
+            nc.vector.quantize_mx(out=words[:, a:b].bitcast(FP8X4), scales=scales[:, a:b], in_=rounded[:, a * PACK : b * PACK])
+            for c, d in WORD_STORES:
+                if d == b:
+                    nc.sync.dma_start(out_words[:, c:d], words[:, c:d].bitcast(I32))
+            for c, d in SCALE_STORES:
+                if d == b:
+                    store_scales(c, d, [nc.scalar] * 4 if d == U else [nc.sync] * 4)
 
-        head = keep.tile([P, PACK, HEAD], F32, name="head")
-        for t in range(PACK):
-            for a in (0, 512):
-                fetch_add(head[:, t, a : a + 512], t, res_head[t][:, a : a + 512], a, a + 512)
-            nc.sync.dma_start(out_rows[:, t, 0:HEAD], head[:, t, :])
-        quantize_out(round_out(head[:, :, 0:512], 0, 512), 0, 512)
-        waiting = [(round_out(head[:, :, 512:HEAD], 512, HEAD), 512, HEAD)]
-        for a, b in TAIL:
+        for a, b in CHUNKS:
             summed = keep.tile([P, PACK, b - a], F32, name="summed_%d" % a)
-            load = a - a % 512
+            load = max(c for c, d in RES_LOADS if c <= a)
             for t in range(PACK):
-                fetch_add(summed[:, t, :], t, res_tail[load][:, t, a - load : b - load], a, b)
-                if t % 2 == 1:
-                    nc.sync.dma_start(out_rows[:, t - 1 : t + 1, a:b], summed[:, t - 1 : t + 1, :])
-            waiting.append((round_out(summed[:], a, b), a, b))
-        for item in waiting:
-            quantize_out(*item)
-        store_scales(0, U, [nc.scalar, nc.sync, nc.scalar, nc.sync])
+                fetch_add(summed[:, t, :], t, res_raw[load][:, t, a - load : b - load], a, b)
+            nc.sync.dma_start(out_rows[:, :, a:b], summed[:])
+            for c, d in ROUNDS:
+                if a <= c < b:
+                    round_out(summed[:, :, c - a : d - a], c, d)
+            if a < QUANTIZE[0][1] <= b:
+                quantize_out(*QUANTIZE[0])
+        for c, d in QUANTIZE[1:]:
+            quantize_out(c, d)

@@ -164,7 +164,7 @@ def tile_picked_unmerge_relu_lo_kernel(tc, xT, w1, res, offs, own, out_0, out_1,
                     nc.sync.dma_start(out_words[:, c:d], words[:, c:d].bitcast(I32))
             for c, d in SCALE_STORES:
                 if d == b:
-                    store_scales(c, d, [nc.scalar] * 4 if d == U else [nc.sync] * 4)
+                    store_scales(c, d, [nc.sync] * 4)
 
         for a, b in CHUNKS:
             summed = keep.tile([P, PACK, b - a], F32, name="summed_%d" % a)

@@ -27,7 +27,7 @@ RES_LOADS = ((0, 512), (512, 768), (768, 1664), (1664, 2048))
 CHUNKS = ((0, 512), (512, 768), (768, 1280), (1280, 1664), (1664, 1920), (1920, 2048))
 ROUNDS = ((0, 512), (512, 768), (768, 1024), (1024, 1280), (1280, 1664), (1664, 1920), (1920, 2048))
 QUANTIZE = ((0, 1024), (1024, 1536), (1536, 1664), (1664, 1920), (1920, 2048))
-WORD_STORES = ((0, 1024), (1024, 1536), (1536, 1920), (1920, 2048))
+WORD_STORES = ((0, 1024), (1024, 1536), (1536, 2048))
 SCALE_STORES = ((0, 1024), (1024, 2048))
 
 

@@ -20,15 +20,23 @@ PACK = 4
 LIST = 16
 LINE = 4
 
-X_LOADS = ((0, 1024), (1024, 1536), (1536, 2048))
-PICKED = ((0, 512), (512, 768), (768, 1024))
-W_LOADS = ((0, 256), (256, 512))
-RES_LOADS = ((0, 512), (512, 768), (768, 1664), (1664, 2048))
-CHUNKS = ((0, 512), (512, 768), (768, 1280), (1280, 1664), (1664, 1920), (1920, 2048))
-ROUNDS = ((0, 512), (512, 768), (768, 1024), (1024, 1280), (1280, 1664), (1664, 1920), (1920, 2048))
-QUANTIZE = ((0, 1024), (1024, 1536), (1536, 1664), (1664, 1920), (1920, 2048))
-WORD_STORES = ((0, 1024), (1024, 1536), (1536, 2048))
-SCALE_STORES = ((0, 1024), (1024, 2048))
+X_LOADS = (
+    (0, 1, 0, 2048),
+    (1, 2, 0, 1024),
+    (1, 2, 1024, 2048),
+    (2, 4, 0, 1024),
+    (2, 3, 1024, 2048),
+    (3, 4, 1024, 1536),
+    (3, 4, 1536, 2048),
+)
+X_TILES = ((0, 0, 2048), (1, 0, 1024), (1, 1024, 2048))
+WOVEN = ((0, 256), (256, 512))
+STEPPED = ((512, 768), (768, 1024))
+LATE_TOKENS = ((512, 768), (768, 896), (896, 1024))
+FIRST_PRODUCTS = WOVEN + LATE_TOKENS
+CHUNKS = ((0, 768), (768, 1152), (1152, 1664), (1664, 1920), (1920, 2048))
+BY_PLANE = 3
+ROUNDS = ((0, 512), (512, 768), (768, 1024), (1024, 1152), (1152, 1664), (1664, 1920), (1920, 2048))
 
 
 def tile_picked_unmerge_relu_lo_kernel(tc, xT, w1, res, offs, own, out_0, out_1, out_2):
@@ -48,85 +56,107 @@ def tile_picked_unmerge_relu_lo_kernel(tc, xT, w1, res, offs, own, out_0, out_1,
         offs_sb = lists.tile([P, S // LIST], U16, name="offs_sb")
         own_sb = lists.tile([P, U // LIST], U16, name="own_sb")
 
-        x_raw = {}
-        for h in range(2):
-            for a, b in X_LOADS:
-                x_raw[h, a] = keep.tile([P, 2, b - a], F32, name="x_raw_%d_%d" % (h, a))
-                nc.sync.dma_start(x_raw[h, a][:], x_rows[:, 2 * h : 2 * h + 2, a:b])
-                if (h, a) == (0, 0):
-                    nc.sync.dma_start(offs_sb[:], offs)
-        w_raw = {}
-        for a, b in W_LOADS:
-            w_raw[a] = keep.tile([P, PACK, b - a], F32, name="w_raw_%d" % a)
-            nc.sync.dma_start(w_raw[a][:], w_rows[:, :, a:b])
+        warm = keep.tile([P, 16], F32, name="warm")
+        nc.vector.memset(warm[:, 0:1], 0.0)
+        nc.scalar.activation(warm[:, 8:9], warm[:, 0:1], RELU)
+
+        x_raw = {(h, a): keep.tile([P, 2, b - a], F32, name="x_raw_%d_%d" % (h, a)) for h, a, b in X_TILES}
+
+        def x_tile(h, a):
+            start = max(c for g, c, d in X_TILES if g == h and c <= a)
+            return x_raw[h, start], start
+
+        for j0, j1, a, b in X_LOADS:
+            if (j0, a) == (2, 0):
+                nc.sync.dma_start(offs_sb[:], offs)
+            raw, start = x_tile(j0 // 2, a)
+            nc.sync.dma_start(raw[:, j0 % 2 : j0 % 2 + j1 - j0, a - start : b - start], x_rows[:, j0:j1, a:b])
+        w_raw = keep.tile([P, PACK, N], F32, name="w_raw")
+        nc.sync.dma_start(w_raw[:], w_rows)
         nc.sync.dma_start(own_sb[:], own)
         res_raw = {}
-        for a, b in RES_LOADS:
-            res_raw[a] = keep.tile([P, PACK, b - a], F32, name="res_raw_%d" % a)
-            nc.sync.dma_start(res_raw[a][:], res_rows[:, :, a:b])
+        for n, (a, b) in enumerate(CHUNKS):
+            if n < BY_PLANE:
+                for t in range(PACK):
+                    res_raw[a, t] = keep.tile([P, b - a], F32, name="res_raw_%d_%d" % (a, t))
+                    nc.sync.dma_start(res_raw[a, t][:], res_rows[:, t, a:b])
+        res_tail = keep.tile([P, PACK, U - CHUNKS[BY_PLANE][0]], F32, name="res_tail")
+        nc.sync.dma_start(res_tail[:], res_rows[:, :, CHUNKS[BY_PLANE][0] :])
 
         pairs = [keep.tile([P, T * 2], BF16, name="pairs_%d" % h) for h in range(2)]
 
-        def cast_pairs(engine, h, load, a, b):
-            src = x_raw[h, load][:, :, a - load : b - load].rearrange("p e (c i) -> p c e i", i=LINE)
+        def cast_pairs(engine, h, a, b):
+            raw, start = x_tile(h, a)
+            src = raw[:, :, a - start : b - start].rearrange("p e (c i) -> p c e i", i=LINE)
             dst = pairs[h][:, 2 * a : 2 * b].rearrange("p (c i e) -> p c e i", i=LINE, e=2)
             if engine == "scalar":
                 nc.scalar.copy(dst, src)
             else:
                 nc.vector.tensor_copy(dst, src)
 
-        picked = [keep.tile([P, (b - a) * PACK], BF16, name="picked_%d" % a, align_bytes=64) for a, b in PICKED]
+        picked = {a: keep.tile([P, (b - a) * PACK], BF16, name="picked_%d" % a, align_bytes=64) for a, b in WOVEN + STEPPED}
+        loose = {a: keep.tile([P, 2, b - a], U32, name="loose_%d" % a) for a, b in WOVEN}
 
-        def gather_pairs(h, n):
-            a, b = PICKED[n]
-            dst = picked[n][:].bitcast(U32).rearrange("p (s h) -> p s h", h=2)[:, :, h]
+        def gather_pairs(h, a, b):
+            if a in loose:
+                dst = loose[a][:, h, :]
+            else:
+                dst = picked[a][:].bitcast(U32).rearrange("p (s h) -> p s h", h=2)[:, :, h]
             nc.vector.tensor_copy(dst, pairs[h][:].bitcast(U32).indirect(offs_sb[:, a // LIST : b // LIST]))
 
-        for h in range(2):
-            cast_pairs("scalar", h, 0, 0, 1024)
-            cast_pairs("vector", h, 1024, 1024, 1536)
-            cast_pairs("vector", h, 1536, 1536, 1888)
-            cast_pairs("scalar", h, 1536, 1888, 2048)
-            if h == 0:
-                for n in range(3):
-                    gather_pairs(0, n)
+        def weave(a):
+            dst = picked[a][:].bitcast(U32).rearrange("p (c i h) -> p c h i", i=2, h=2)
+            nc.scalar.copy(dst, loose[a][:].rearrange("p h (c i) -> p c h i", i=2))
 
-        w_first = keep.tile([P, P * PACK], BF16, name="w_first", tag="shared", align_bytes=64)
-        w_rest = keep.tile([P, 3 * P * PACK], BF16, name="w_rest", align_bytes=64)
+        cast_pairs("scalar", 0, 0, 640)
+        cast_pairs("vector", 0, 640, 1024)
+        cast_pairs("vector", 0, 1024, 1728)
+        cast_pairs("scalar", 0, 1728, 2048)
+        for a, b in WOVEN + STEPPED:
+            gather_pairs(0, a, b)
+        cast_pairs("scalar", 1, 0, 1024)
+        cast_pairs("vector", 1, 1024, 1536)
+        cast_pairs("vector", 1, 1536, 1888)
+        cast_pairs("scalar", 1, 1888, 2048)
+        for a, b in WOVEN:
+            gather_pairs(1, a, b)
+            weave(a)
+
+        w_dealt = [keep.tile([P, 2 * P * PACK], BF16, name="w_dealt_%d" % u, tag="w_dealt_%d" % u, align_bytes=64) for u in range(2)]
         w_codes = keep.tile([P, N], U32, name="w_codes", align_bytes=64)
         w_scales = keep.tile([P, N], U8, name="w_scales", align_bytes=64)
-        for a, b in W_LOADS:
-            src = w_raw[a][:].rearrange("p j (m t) -> p m j t", t=PACK)
-            m0, m1 = a // PACK, b // PACK
-            nc.scalar.copy(w_first[:].rearrange("p (m j) -> p m j", j=PACK)[:, m0:m1, :], src[:, :, :, 0])
-            nc.scalar.copy(w_rest[:].rearrange("p (t m j) -> p m j t", t=3, j=PACK)[:, m0:m1, :, :], src[:, :, :, 1:PACK])
+        for u in range(2):
+            src = w_raw[:].rearrange("p j (m t) -> p m j t", t=PACK)[:, :, :, 2 * u : 2 * u + 2]
+            nc.scalar.copy(w_dealt[u][:].rearrange("p (t m j) -> p m j t", t=2, j=PACK), src)
 
-        x_codes = [None, None]
+        def quantize_w(t0, t1):
+            src = w_dealt[t0 // 2][:, t0 % 2 * P * PACK : (t0 % 2 + t1 - t0) * P * PACK]
+            nc.vector.quantize_mx(out=w_codes[:, t0 * P : t1 * P].bitcast(FP8X4), scales=w_scales[:, t0 * P : t1 * P], in_=src)
+
+        x_low = keep.tile([P, 512], U32, name="x_low", align_bytes=64)
+        x_codes = [x_low]
         x_scales = [keep.tile([P, 512], U8, name="x_scales_%d" % a, align_bytes=64) for a in (0, 512)]
 
-        def quantize_x(n):
-            a, b = PICKED[n]
+        def quantize_x(a, b):
             cols = slice(a % 512, a % 512 + b - a)
-            nc.vector.quantize_mx(out=x_codes[a // 512][:, cols].bitcast(FP8X4), scales=x_scales[a // 512][:, cols], in_=picked[n][:])
+            first = a // 256 * 256
+            src = picked[first][:, (a - first) * PACK : (b - first) * PACK]
+            nc.vector.quantize_mx(out=x_codes[a // 512][:, cols].bitcast(FP8X4), scales=x_scales[a // 512][:, cols], in_=src)
 
-        x_codes[0] = keep.tile([P, 512], U32, name="x_codes_0", align_bytes=64)
-        gather_pairs(1, 0)
-        gather_pairs(1, 1)
-        quantize_x(0)
-        gather_pairs(1, 2)
-        nc.vector.quantize_mx(out=w_codes[:, 0:P].bitcast(FP8X4), scales=w_scales[:, 0:P], in_=w_first[:])
-        x_codes[1] = keep.tile([P, 512], U32, name="x_codes_1", tag="shared", align_bytes=64)
-        quantize_x(1)
-        quantize_x(2)
-        nc.vector.quantize_mx(out=w_codes[:, P : 2 * P].bitcast(FP8X4), scales=w_scales[:, P : 2 * P], in_=w_rest[:, 0 : P * PACK])
-        nc.vector.quantize_mx(out=w_codes[:, 2 * P :].bitcast(FP8X4), scales=w_scales[:, 2 * P :], in_=w_rest[:, P * PACK :])
+        for a, b in STEPPED:
+            gather_pairs(1, a, b)
+        for a, b in WOVEN:
+            quantize_x(a, b)
+        quantize_w(0, 2)
+        x_codes.append(keep.tile([P, 512], U32, name="x_high", tag="w_dealt_0", align_bytes=64))
+        for a, b in LATE_TOKENS:
+            quantize_x(a, b)
+        quantize_w(2, 4)
 
         y = []
         for t in range(PACK):
             y.append(keep.tile([P, S], F32, name="y_%d" % t))
-            width = 256 if t == 0 else 512
-            for a in range(0, S, width):
-                b = a + width
+            for a, b in FIRST_PRODUCTS if t == 0 else ((0, 512), (512, 1024)):
                 acc = psum.tile([P, 512], F32, name="acc")
                 cols = slice(a % 512, a % 512 + b - a)
                 nc.tensor.matmul_mx(
@@ -138,7 +168,10 @@ def tile_picked_unmerge_relu_lo_kernel(tc, xT, w1, res, offs, own, out_0, out_1,
                     start=True,
                     stop=True,
                 )
-                nc.scalar.activation(y[t][:, a:b], acc[:, 0 : b - a], RELU)
+                if (t, a) == (0, 512):
+                    nc.vector.tensor_scalar_max(y[t][:, a:b], acc[:, 0 : b - a], 0.0)
+                else:
+                    nc.scalar.activation(y[t][:, a:b], acc[:, 0 : b - a], RELU)
 
         scales = keep.tile([P, U], U8, name="scales", align_bytes=64)
 
@@ -159,23 +192,31 @@ def tile_picked_unmerge_relu_lo_kernel(tc, xT, w1, res, offs, own, out_0, out_1,
 
         def quantize_out(a, b):
             nc.vector.quantize_mx(out=words[:, a:b].bitcast(FP8X4), scales=scales[:, a:b], in_=rounded[:, a * PACK : b * PACK])
-            for c, d in WORD_STORES:
-                if d == b:
-                    nc.sync.dma_start(out_words[:, c:d], words[:, c:d].bitcast(I32))
-            for c, d in SCALE_STORES:
-                if d == b:
-                    store_scales(c, d, [nc.sync] * 4)
 
-        for a, b in CHUNKS:
+        def store_words(a, b):
+            nc.sync.dma_start(out_words[:, a:b], words[:, a:b].bitcast(I32))
+
+        for n, (a, b) in enumerate(CHUNKS):
             summed = keep.tile([P, PACK, b - a], F32, name="summed_%d" % a)
-            load = max(c for c, d in RES_LOADS if c <= a)
             for t in range(PACK):
-                fetch_add(summed[:, t, :], t, res_raw[load][:, t, a - load : b - load], a, b)
-            nc.sync.dma_start(out_rows[:, :, a:b], summed[:])
+                if n < BY_PLANE:
+                    residual = res_raw[a, t][:]
+                else:
+                    residual = res_tail[:, t, a - CHUNKS[BY_PLANE][0] : b - CHUNKS[BY_PLANE][0]]
+                fetch_add(summed[:, t, :], t, residual, a, b)
+                if n < BY_PLANE:
+                    nc.sync.dma_start(out_rows[:, t, a:b], summed[:, t, :])
+                elif t % 2 == 1:
+                    if (n, t) == (4, 1):
+                        store_words(768, 1152)
+                    nc.sync.dma_start(out_rows[:, t - 1 : t + 1, a:b], summed[:, t - 1 : t + 1, :])
+                if (n, t) == (2, 3):
+                    store_words(0, 768)
+                    store_scales(0, 768, [nc.sync] * 4)
             for c, d in ROUNDS:
                 if a <= c < b:
                     round_out(summed[:, :, c - a : d - a], c, d)
-            if a < QUANTIZE[0][1] <= b:
-                quantize_out(*QUANTIZE[0])
-        for c, d in QUANTIZE[1:]:
-            quantize_out(c, d)
+                    quantize_out(c, d)
+        store_words(1152, 1664)
+        store_words(1664, 2048)
+        store_scales(768, U, [nc.sync] * 4)

@@ -75,13 +75,18 @@ def tile_picked_unmerge_relu_lo_kernel(tc, xT, w1, res, offs, own, out_0, out_1,
         nc.sync.dma_start(w_raw[:], w_rows)
         nc.sync.dma_start(own_sb[:], own)
         res_raw = {}
-        for n, (a, b) in enumerate(CHUNKS):
-            if n < BY_PLANE:
+        for a, b in CHUNKS[:2]:
+            for t in range(PACK):
+                res_raw[a, t] = keep.tile([P, b - a], F32, name="res_raw_%d_%d" % (a, t), tag="res_raw_%d_%d" % (a, t))
+                nc.sync.dma_start(res_raw[a, t][:], res_rows[:, t, a:b])
+
+        def load_res(chunks, tag):
+            first, last = chunks[0][0], chunks[-1][1]
+            whole = keep.tile([P, PACK, last - first], F32, name="res_raw_%d" % first, tag=tag)
+            nc.sync.dma_start(whole[:], res_rows[:, :, first:last])
+            for a, b in chunks:
                 for t in range(PACK):
-                    res_raw[a, t] = keep.tile([P, b - a], F32, name="res_raw_%d_%d" % (a, t))
-                    nc.sync.dma_start(res_raw[a, t][:], res_rows[:, t, a:b])
-        res_tail = keep.tile([P, PACK, U - CHUNKS[BY_PLANE][0]], F32, name="res_tail")
-        nc.sync.dma_start(res_tail[:], res_rows[:, :, CHUNKS[BY_PLANE][0] :])
+                    res_raw[a, t] = whole[:, t, a - first : b - first]
 
         pairs = [keep.tile([P, T * 2], BF16, name="pairs_%d" % h) for h in range(2)]
 
@@ -147,7 +152,8 @@ def tile_picked_unmerge_relu_lo_kernel(tc, xT, w1, res, offs, own, out_0, out_1,
             gather_pairs(1, a, b)
         for a, b in WOVEN:
             quantize_x(a, b)
-        quantize_w(0, 2)
+        quantize_w(0, 1)
+        quantize_w(1, 2)
         x_codes.append(keep.tile([P, 512], U32, name="x_high", tag="w_dealt_0", align_bytes=64))
         for a, b in LATE_TOKENS:
             quantize_x(a, b)
@@ -199,24 +205,24 @@ def tile_picked_unmerge_relu_lo_kernel(tc, xT, w1, res, offs, own, out_0, out_1,
         for n, (a, b) in enumerate(CHUNKS):
             summed = keep.tile([P, PACK, b - a], F32, name="summed_%d" % a)
             for t in range(PACK):
-                if n < BY_PLANE:
-                    residual = res_raw[a, t][:]
-                else:
-                    residual = res_tail[:, t, a - CHUNKS[BY_PLANE][0] : b - CHUNKS[BY_PLANE][0]]
-                fetch_add(summed[:, t, :], t, residual, a, b)
+                fetch_add(summed[:, t, :], t, res_raw[a, t][:], a, b)
+                if (n, t) == (0, 0):
+                    load_res(CHUNKS[2:3], "res_raw_%d_%d" % (a, t))
+                if (n, t) == (0, 2):
+                    load_res(CHUNKS[3:], "res_raw_%d_%d" % (a, t))
                 if n < BY_PLANE:
                     nc.sync.dma_start(out_rows[:, t, a:b], summed[:, t, :])
                 elif t % 2 == 1:
-                    if (n, t) == (4, 1):
-                        store_words(768, 1152)
                     nc.sync.dma_start(out_rows[:, t - 1 : t + 1, a:b], summed[:, t - 1 : t + 1, :])
-                if (n, t) == (2, 3):
+                if (n, t) == (2, 0):
                     store_words(0, 768)
-                    store_scales(0, 768, [nc.sync] * 4)
+                if (n, t) == (2, 3):
+                    store_words(768, 1152)
+                    store_scales(0, 1152, [nc.sync] * 4)
             for c, d in ROUNDS:
                 if a <= c < b:
                     round_out(summed[:, :, c - a : d - a], c, d)
                     quantize_out(c, d)
         store_words(1152, 1664)
         store_words(1664, 2048)
-        store_scales(768, U, [nc.sync] * 4)
+        store_scales(1152, U, [nc.sync] * 4)

@@ -12,6 +12,7 @@ I32 = mybir.dt.int32
 U16 = mybir.dt.uint16
 U8 = mybir.dt.uint8
 FP8X4 = mybir.dt.float8_e4m3fn_x4
+COPY = mybir.ActivationFunctionType.Copy
 RELU = mybir.ActivationFunctionType.Relu
 ADD = mybir.AluOpType.add
 
@@ -20,20 +21,11 @@ PACK = 4
 LIST = 16
 LINE = 4
 
-X_LOADS = (
-    (0, 1, 0, 2048),
-    (1, 2, 0, 1024),
-    (1, 2, 1024, 2048),
-    (2, 4, 0, 1024),
-    (2, 3, 1024, 2048),
-    (3, 4, 1024, 1536),
-    (3, 4, 1536, 2048),
-)
-X_TILES = ((0, 0, 2048), (1, 0, 1024), (1, 1024, 2048))
-WOVEN = ((0, 256), (256, 512))
-STEPPED = ((512, 768), (768, 1024))
-LATE_TOKENS = ((512, 768), (768, 896), (896, 1024))
-FIRST_PRODUCTS = WOVEN + LATE_TOKENS
+X_LOADS = tuple((j, a, a + 1024) for j in range(3) for a in (0, 1024)) + ((3, 0, 1024), (3, 1024, 1536), (3, 1536, 2048))
+VECTOR_TOKENS = (0, 352)
+SCALAR_TOKENS = ((352, 608), (608, 1024))
+EARLY = 512
+FIRST_PRODUCTS = ((0, 256), (256, 512), (512, 768), (768, 896), (896, 1024))
 CHUNKS = ((0, 768), (768, 1152), (1152, 1664), (1664, 1920), (1920, 2048))
 BY_PLANE = 3
 ROUNDS = ((0, 512), (512, 768), (768, 1024), (1024, 1152), (1152, 1664), (1664, 1920), (1920, 2048))
@@ -60,17 +52,11 @@ def tile_picked_unmerge_relu_lo_kernel(tc, xT, w1, res, offs, own, out_0, out_1,
         nc.vector.memset(warm[:, 0:1], 0.0)
         nc.scalar.activation(warm[:, 8:9], warm[:, 0:1], RELU)
 
-        x_raw = {(h, a): keep.tile([P, 2, b - a], F32, name="x_raw_%d_%d" % (h, a)) for h, a, b in X_TILES}
-
-        def x_tile(h, a):
-            start = max(c for g, c, d in X_TILES if g == h and c <= a)
-            return x_raw[h, start], start
-
-        for j0, j1, a, b in X_LOADS:
-            if (j0, a) == (2, 0):
+        x_raw = [keep.tile([P, T], F32, name="x_raw_%d" % j) for j in range(PACK)]
+        for j, a, b in X_LOADS:
+            nc.sync.dma_start(x_raw[j][:, a:b], x_rows[:, j, a:b])
+            if (j, a) == (0, 0):
                 nc.sync.dma_start(offs_sb[:], offs)
-            raw, start = x_tile(j0 // 2, a)
-            nc.sync.dma_start(raw[:, j0 % 2 : j0 % 2 + j1 - j0, a - start : b - start], x_rows[:, j0:j1, a:b])
         w_raw = keep.tile([P, PACK, N], F32, name="w_raw")
         nc.sync.dma_start(w_raw[:], w_rows)
         nc.sync.dma_start(own_sb[:], own)
@@ -88,92 +74,72 @@ def tile_picked_unmerge_relu_lo_kernel(tc, xT, w1, res, offs, own, out_0, out_1,
                 for t in range(PACK):
                     res_raw[a, t] = whole[:, t, a - first : b - first]
 
-        pairs = [keep.tile([P, T * 2], BF16, name="pairs_%d" % h) for h in range(2)]
+        x_half = [keep.tile([P, T], BF16, name="x_half_%d" % j) for j in range(PACK)]
+        picked = keep.tile([P, S * PACK], BF16, name="picked", align_bytes=64)
 
-        def cast_pairs(engine, h, a, b):
-            raw, start = x_tile(h, a)
-            src = raw[:, :, a - start : b - start].rearrange("p e (c i) -> p c e i", i=LINE)
-            dst = pairs[h][:, 2 * a : 2 * b].rearrange("p (c i e) -> p c e i", i=LINE, e=2)
-            if engine == "scalar":
-                nc.scalar.copy(dst, src)
-            else:
-                nc.vector.tensor_copy(dst, src)
+        def picked_plane(j, a, b):
+            return picked[:].rearrange("p (s j) -> p s j", j=PACK)[:, a:b, j]
 
-        picked = {a: keep.tile([P, (b - a) * PACK], BF16, name="picked_%d" % a, align_bytes=64) for a, b in WOVEN + STEPPED}
-        loose = {a: keep.tile([P, 2, b - a], U32, name="loose_%d" % a) for a, b in WOVEN}
-
-        def gather_pairs(h, a, b):
-            if a in loose:
-                dst = loose[a][:, h, :]
-            else:
-                dst = picked[a][:].bitcast(U32).rearrange("p (s h) -> p s h", h=2)[:, :, h]
-            nc.vector.tensor_copy(dst, pairs[h][:].bitcast(U32).indirect(offs_sb[:, a // LIST : b // LIST]))
-
-        def weave(a):
-            dst = picked[a][:].bitcast(U32).rearrange("p (c i h) -> p c h i", i=2, h=2)
-            nc.scalar.copy(dst, loose[a][:].rearrange("p h (c i) -> p c h i", i=2))
-
-        cast_pairs("scalar", 0, 0, 640)
-        cast_pairs("vector", 0, 640, 1024)
-        cast_pairs("vector", 0, 1024, 1728)
-        cast_pairs("scalar", 0, 1728, 2048)
-        for a, b in WOVEN + STEPPED:
-            gather_pairs(0, a, b)
-        cast_pairs("scalar", 1, 0, 1024)
-        cast_pairs("vector", 1, 1024, 1536)
-        cast_pairs("vector", 1, 1536, 1888)
-        cast_pairs("scalar", 1, 1888, 2048)
-        for a, b in WOVEN:
-            gather_pairs(1, a, b)
-            weave(a)
+        for j in range(PACK):
+            for i, a, b in X_LOADS:
+                if i == j:
+                    nc.vector.tensor_copy(x_half[j][:, a:b], x_raw[j][:, a:b])
+            a, b = VECTOR_TOKENS
+            nc.vector.tensor_copy(picked_plane(j, a, b), x_raw[j][:].indirect(offs_sb[:, a // LIST : b // LIST]))
+            for a, b in SCALAR_TOKENS:
+                nc.scalar.activation(picked_plane(j, a, b), x_half[j][:].indirect(offs_sb[:, a // LIST : b // LIST]), COPY)
 
         w_dealt = [keep.tile([P, 2 * P * PACK], BF16, name="w_dealt_%d" % u, tag="w_dealt_%d" % u, align_bytes=64) for u in range(2)]
         w_codes = keep.tile([P, N], U32, name="w_codes", align_bytes=64)
         w_scales = keep.tile([P, N], U8, name="w_scales", align_bytes=64)
-        for u in range(2):
+
+        def deal(copy, u):
             src = w_raw[:].rearrange("p j (m t) -> p m j t", t=PACK)[:, :, :, 2 * u : 2 * u + 2]
-            nc.scalar.copy(w_dealt[u][:].rearrange("p (t m j) -> p m j t", t=2, j=PACK), src)
+            copy(w_dealt[u][:].rearrange("p (t m j) -> p m j t", t=2, j=PACK), src)
 
         def quantize_w(t0, t1):
             src = w_dealt[t0 // 2][:, t0 % 2 * P * PACK : (t0 % 2 + t1 - t0) * P * PACK]
             nc.vector.quantize_mx(out=w_codes[:, t0 * P : t1 * P].bitcast(FP8X4), scales=w_scales[:, t0 * P : t1 * P], in_=src)
 
-        x_low = keep.tile([P, 512], U32, name="x_low", align_bytes=64)
-        x_codes = [x_low]
-        x_scales = [keep.tile([P, 512], U8, name="x_scales_%d" % a, align_bytes=64) for a in (0, 512)]
+        x_codes = [keep.tile([P, EARLY], U32, name="x_low", align_bytes=64)]
+        x_scales = [keep.tile([P, n], U8, name="x_scales_%d" % a, align_bytes=64) for a, n in ((0, EARLY), (EARLY, S - EARLY))]
 
         def quantize_x(a, b):
-            cols = slice(a % 512, a % 512 + b - a)
-            first = a // 256 * 256
-            src = picked[first][:, (a - first) * PACK : (b - first) * PACK]
-            nc.vector.quantize_mx(out=x_codes[a // 512][:, cols].bitcast(FP8X4), scales=x_scales[a // 512][:, cols], in_=src)
+            first = a // EARLY * EARLY
+            cols = slice(a - first, b - first)
+            src = picked[:, a * PACK : b * PACK]
+            nc.vector.quantize_mx(out=x_codes[a // EARLY][:, cols].bitcast(FP8X4), scales=x_scales[a // EARLY][:, cols], in_=src)
 
-        for a, b in STEPPED:
-            gather_pairs(1, a, b)
-        for a, b in WOVEN:
+        for a, b in FIRST_PRODUCTS[:2]:
             quantize_x(a, b)
+        deal(nc.vector.tensor_copy, 0)
+        deal(nc.scalar.copy, 1)
         quantize_w(0, 1)
         quantize_w(1, 2)
-        x_codes.append(keep.tile([P, 512], U32, name="x_high", tag="w_dealt_0", align_bytes=64))
-        for a, b in LATE_TOKENS:
+        x_codes.append(keep.tile([P, S - EARLY], U32, name="x_high", tag="w_dealt_0", align_bytes=64))
+        for a, b in FIRST_PRODUCTS[2:]:
             quantize_x(a, b)
         quantize_w(2, 4)
+
+        def product(out, t, a, b):
+            first = a // EARLY * EARLY
+            cols = slice(a - first, b - first)
+            nc.tensor.matmul_mx(
+                out=out,
+                lhsT=w_codes[:, t * P : (t + 1) * P].bitcast(FP8X4),
+                lhsT_scale=w_scales[:, t * P : (t + 1) * P],
+                rhs=x_codes[a // EARLY][:, cols].bitcast(FP8X4),
+                rhs_scale=x_scales[a // EARLY][:, cols],
+                start=True,
+                stop=True,
+            )
 
         y = []
         for t in range(PACK):
             y.append(keep.tile([P, S], F32, name="y_%d" % t))
             for a, b in FIRST_PRODUCTS if t == 0 else ((0, 512), (512, 1024)):
                 acc = psum.tile([P, 512], F32, name="acc")
-                cols = slice(a % 512, a % 512 + b - a)
-                nc.tensor.matmul_mx(
-                    out=acc[:, 0 : b - a],
-                    lhsT=w_codes[:, t * P : (t + 1) * P].bitcast(FP8X4),
-                    lhsT_scale=w_scales[:, t * P : (t + 1) * P],
-                    rhs=x_codes[a // 512][:, cols].bitcast(FP8X4),
-                    rhs_scale=x_scales[a // 512][:, cols],
-                    start=True,
-                    stop=True,
-                )
+                product(acc[:, 0 : b - a], t, a, b)
                 if (t, a) == (0, 512):
                     nc.vector.tensor_scalar_max(y[t][:, a:b], acc[:, 0 : b - a], 0.0)
                 else:
@@ -210,7 +176,7 @@ def tile_picked_unmerge_relu_lo_kernel(tc, xT, w1, res, offs, own, out_0, out_1,
                     load_res(CHUNKS[2:3], "res_raw_%d_%d" % (a, t))
                 if (n, t) == (0, 2):
                     load_res(CHUNKS[3:], "res_raw_%d_%d" % (a, t))
-                if n < BY_PLANE:
+                if n < BY_PLANE and n != 1:
                     nc.sync.dma_start(out_rows[:, t, a:b], summed[:, t, :])
                 elif t % 2 == 1:
                     nc.sync.dma_start(out_rows[:, t - 1 : t + 1, a:b], summed[:, t - 1 : t + 1, :])

@@ -150,6 +150,11 @@ def tile_picked_unmerge_relu_lo_kernel(tc, xT, w1, res, offs, own, out_0, out_1,
         def fetch_add(dst, t, residual, a, b):
             nc.vector.tensor_tensor(dst, y[t][:].indirect(own_sb[:, a // LIST : b // LIST]), residual, ADD)
 
+        fetched = {}
+        for a, b in CHUNKS:
+            fetched[a] = keep.tile([P, b - a], F32, name="fetched_%d" % a)
+            nc.scalar.activation(fetched[a][:], y[PACK - 1][:].indirect(own_sb[:, a // LIST : b // LIST]), COPY)
+
         rounded = keep.tile([P, U * PACK], BF16, name="rounded", align_bytes=64)
 
         def round_out(summed, a, b):
@@ -171,7 +176,10 @@ def tile_picked_unmerge_relu_lo_kernel(tc, xT, w1, res, offs, own, out_0, out_1,
         for n, (a, b) in enumerate(CHUNKS):
             summed = keep.tile([P, PACK, b - a], F32, name="summed_%d" % a)
             for t in range(PACK):
-                fetch_add(summed[:, t, :], t, res_raw[a, t][:], a, b)
+                if t == PACK - 1:
+                    nc.vector.tensor_tensor(summed[:, t, :], fetched[a][:], res_raw[a, t][:], ADD)
+                else:
+                    fetch_add(summed[:, t, :], t, res_raw[a, t][:], a, b)
                 if (n, t) == (0, 0):
                     load_res(CHUNKS[2:3], "res_raw_%d_%d" % (a, t))
                 if (n, t) == (0, 2):

@@ -26,9 +26,7 @@ VECTOR_TOKENS = (0, 352)
 SCALAR_TOKENS = ((352, 608), (608, 1024))
 EARLY = 512
 FIRST_PRODUCTS = ((0, 256), (256, 512), (512, 768), (768, 896), (896, 1024))
-CHUNKS = ((0, 768), (768, 1152), (1152, 1664), (1664, 1920), (1920, 2048))
-BY_PLANE = 3
-ROUNDS = ((0, 512), (512, 768), (768, 1024), (1024, 1152), (1152, 1664), (1664, 1920), (1920, 2048))
+FIRST, SECOND, SHARED, LAST = (0, 768), (768, 1152), (1152, 1792), (1792, 2048)
 
 
 def tile_picked_unmerge_relu_lo_kernel(tc, xT, w1, res, offs, own, out_0, out_1, out_2):
@@ -61,18 +59,16 @@ def tile_picked_unmerge_relu_lo_kernel(tc, xT, w1, res, offs, own, out_0, out_1,
         nc.sync.dma_start(w_raw[:], w_rows)
         nc.sync.dma_start(own_sb[:], own)
         res_raw = {}
-        for a, b in CHUNKS[:2]:
-            for t in range(PACK):
-                res_raw[a, t] = keep.tile([P, b - a], F32, name="res_raw_%d_%d" % (a, t), tag="res_raw_%d_%d" % (a, t))
-                nc.sync.dma_start(res_raw[a, t][:], res_rows[:, t, a:b])
+        for (a, b), groups in ((FIRST, ((0, 1), (1, 2), (2, 4))), (SECOND, ((0, 4),)), (SHARED, ((0, 4),)), (LAST, ((0, 4),))):
+            for t0, t1 in groups:
+                part = keep.tile([P, t1 - t0, b - a], F32, name="res_%d_%d" % (a, t0))
+                nc.sync.dma_start(part[:], res_rows[:, t0:t1, a:b])
+                for t in range(t0, t1):
+                    res_raw[a, t] = (part, t - t0)
 
-        def load_res(chunks, tag):
-            first, last = chunks[0][0], chunks[-1][1]
-            whole = keep.tile([P, PACK, last - first], F32, name="res_raw_%d" % first, tag=tag)
-            nc.sync.dma_start(whole[:], res_rows[:, :, first:last])
-            for a, b in chunks:
-                for t in range(PACK):
-                    res_raw[a, t] = whole[:, t, a - first : b - first]
+        def residual(t0, t1, a):
+            part, t = res_raw[a, t0]
+            return part[:, t : t + t1 - t0, :]
 
         x_half = [keep.tile([P, T], BF16, name="x_half_%d" % j) for j in range(PACK)]
         picked = keep.tile([P, S * PACK], BF16, name="picked", align_bytes=64)
@@ -147,13 +143,10 @@ def tile_picked_unmerge_relu_lo_kernel(tc, xT, w1, res, offs, own, out_0, out_1,
 
         scales = keep.tile([P, U], U8, name="scales", align_bytes=64)
 
-        def fetch_add(dst, t, residual, a, b):
-            nc.vector.tensor_tensor(dst, y[t][:].indirect(own_sb[:, a // LIST : b // LIST]), residual, ADD)
-
-        fetched = {}
-        for a, b in CHUNKS:
-            fetched[a] = keep.tile([P, b - a], F32, name="fetched_%d" % a)
-            nc.scalar.activation(fetched[a][:], y[PACK - 1][:].indirect(own_sb[:, a // LIST : b // LIST]), COPY)
+        a, b = SHARED
+        fetched = [keep.tile([P, 2, b - a], F32, name="fetched_%d" % u) for u in range(2)]
+        for t in range(PACK):
+            nc.scalar.activation(fetched[t // 2][:, t % 2, :], y[t][:].indirect(own_sb[:, a // LIST : b // LIST]), COPY)
 
         rounded = keep.tile([P, U * PACK], BF16, name="rounded", align_bytes=64)
 
@@ -173,30 +166,49 @@ def tile_picked_unmerge_relu_lo_kernel(tc, xT, w1, res, offs, own, out_0, out_1,
         def store_words(a, b):
             nc.sync.dma_start(out_words[:, a:b], words[:, a:b].bitcast(I32))
 
-        for n, (a, b) in enumerate(CHUNKS):
-            summed = keep.tile([P, PACK, b - a], F32, name="summed_%d" % a)
+        summed = {}
+
+        def store_out(chunk, t0, t1):
+            a, b = chunk
+            nc.sync.dma_start(out_rows[:, t0:t1, a:b], summed[a][:, t0:t1, :])
+
+        def fetch_add(chunk, stores):
+            a, b = chunk
+            summed[a] = keep.tile([P, PACK, b - a], F32, name="summed_%d" % a)
             for t in range(PACK):
-                if t == PACK - 1:
-                    nc.vector.tensor_tensor(summed[:, t, :], fetched[a][:], res_raw[a, t][:], ADD)
-                else:
-                    fetch_add(summed[:, t, :], t, res_raw[a, t][:], a, b)
-                if (n, t) == (0, 0):
-                    load_res(CHUNKS[2:3], "res_raw_%d_%d" % (a, t))
-                if (n, t) == (0, 2):
-                    load_res(CHUNKS[3:], "res_raw_%d_%d" % (a, t))
-                if n < BY_PLANE and n != 1:
-                    nc.sync.dma_start(out_rows[:, t, a:b], summed[:, t, :])
-                elif t % 2 == 1:
-                    nc.sync.dma_start(out_rows[:, t - 1 : t + 1, a:b], summed[:, t - 1 : t + 1, :])
-                if (n, t) == (2, 0):
-                    store_words(0, 768)
-                if (n, t) == (2, 3):
-                    store_words(768, 1152)
-                    store_scales(0, 1152, [nc.sync] * 4)
-            for c, d in ROUNDS:
-                if a <= c < b:
-                    round_out(summed[:, :, c - a : d - a], c, d)
-                    quantize_out(c, d)
-        store_words(1152, 1664)
-        store_words(1664, 2048)
-        store_scales(1152, U, [nc.sync] * 4)
+                src = residual(t, t + 1, a)[:, 0, :]
+                nc.vector.tensor_tensor(summed[a][:, t, :], y[t][:].indirect(own_sb[:, a // LIST : b // LIST]), src, ADD)
+                for t0, t1 in stores:
+                    if t1 == t + 1:
+                        store_out(chunk, t0, t1)
+
+        def round_range(chunk, c, d):
+            a, b = chunk
+            round_out(summed[a][:, :, c - a : d - a], c, d)
+
+        fetch_add(FIRST, ((0, 1), (1, 2), (2, 3), (3, 4)))
+        round_range(FIRST, 0, 512)
+        round_range(FIRST, 512, 768)
+        fetch_add(SECOND, ((0, 2), (2, 4)))
+        round_range(SECOND, *SECOND)
+        a, b = SHARED
+        summed[a] = keep.tile([P, PACK, b - a], F32, name="summed_%d" % a)
+        for u in range(2):
+            nc.vector.tensor_tensor(summed[a][:, 2 * u : 2 * u + 2, :], fetched[u][:], residual(2 * u, 2 * u + 2, a), ADD)
+            store_out(SHARED, 2 * u, 2 * u + 2)
+        round_range(SHARED, 1152, 1536)
+        round_range(SHARED, 1536, 1792)
+        quantize_out(0, 512)
+        quantize_out(512, 768)
+        store_words(0, 768)
+        store_scales(0, 768, [nc.sync] * 4)
+        fetch_add(LAST, ((0, 2), (2, 4)))
+        quantize_out(*SECOND)
+        store_words(*SECOND)
+        round_range(LAST, *LAST)
+        quantize_out(1152, 1536)
+        quantize_out(1536, 1792)
+        store_words(*SHARED)
+        quantize_out(*LAST)
+        store_words(*LAST)
+        store_scales(768, U, [nc.sync] * 4)

@@ -26,7 +26,7 @@ VECTOR_TOKENS = (0, 352)
 SCALAR_TOKENS = ((352, 608), (608, 1024))
 EARLY = 512
 FIRST_PRODUCTS = ((0, 256), (256, 512), (512, 768), (768, 896), (896, 1024))
-FIRST, SECOND, SHARED, LAST = (0, 768), (768, 1152), (1152, 1792), (1792, 2048)
+FIRST, SECOND, SHARED, LAST = (0, 832), (1472, 1920), (832, 1472), (1920, 2048)
 
 
 def tile_picked_unmerge_relu_lo_kernel(tc, xT, w1, res, offs, own, out_0, out_1, out_2):
@@ -59,12 +59,16 @@ def tile_picked_unmerge_relu_lo_kernel(tc, xT, w1, res, offs, own, out_0, out_1,
         nc.sync.dma_start(w_raw[:], w_rows)
         nc.sync.dma_start(own_sb[:], own)
         res_raw = {}
-        for (a, b), groups in ((FIRST, ((0, 1), (1, 2), (2, 4))), (SECOND, ((0, 4),)), (SHARED, ((0, 4),)), (LAST, ((0, 4),))):
-            for t0, t1 in groups:
-                part = keep.tile([P, t1 - t0, b - a], F32, name="res_%d_%d" % (a, t0))
-                nc.sync.dma_start(part[:], res_rows[:, t0:t1, a:b])
-                for t in range(t0, t1):
-                    res_raw[a, t] = (part, t - t0)
+
+        def load_res(chunk, t0, t1, tag):
+            a, b = chunk
+            part = keep.tile([P, t1 - t0, b - a], F32, name="res_%d_%d" % (a, t0), tag=tag)
+            nc.sync.dma_start(part[:], res_rows[:, t0:t1, a:b])
+            for t in range(t0, t1):
+                res_raw[a, t] = (part, t - t0)
+
+        for chunk, t0, t1 in ((FIRST, 0, 2), (FIRST, 2, 4), (SECOND, 0, 1), (SHARED, 0, 4), (SECOND, 1, 4)):
+            load_res(chunk, t0, t1, "res_%d_%d" % (chunk[0], t0))
 
         def residual(t0, t1, a):
             part, t = res_raw[a, t0]
@@ -144,7 +148,7 @@ def tile_picked_unmerge_relu_lo_kernel(tc, xT, w1, res, offs, own, out_0, out_1,
         scales = keep.tile([P, U], U8, name="scales", align_bytes=64)
 
         a, b = SHARED
-        fetched = [keep.tile([P, 2, b - a], F32, name="fetched_%d" % u) for u in range(2)]
+        fetched = [keep.tile([P, 2, b - a], F32, name="fetched_%d" % u, tag="fetched_%d" % u) for u in range(2)]
         for t in range(PACK):
             nc.scalar.activation(fetched[t // 2][:, t % 2, :], y[t][:].indirect(own_sb[:, a // LIST : b // LIST]), COPY)
 
@@ -172,43 +176,49 @@ def tile_picked_unmerge_relu_lo_kernel(tc, xT, w1, res, offs, own, out_0, out_1,
             a, b = chunk
             nc.sync.dma_start(out_rows[:, t0:t1, a:b], summed[a][:, t0:t1, :])
 
-        def fetch_add(chunk, stores):
+        def fetch_add(chunk, t):
             a, b = chunk
-            summed[a] = keep.tile([P, PACK, b - a], F32, name="summed_%d" % a)
-            for t in range(PACK):
-                src = residual(t, t + 1, a)[:, 0, :]
-                nc.vector.tensor_tensor(summed[a][:, t, :], y[t][:].indirect(own_sb[:, a // LIST : b // LIST]), src, ADD)
-                for t0, t1 in stores:
-                    if t1 == t + 1:
-                        store_out(chunk, t0, t1)
+            nc.vector.tensor_tensor(summed[a][:, t, :], y[t][:].indirect(own_sb[:, a // LIST : b // LIST]), residual(t, t + 1, a)[:, 0, :], ADD)
 
         def round_range(chunk, c, d):
             a, b = chunk
             round_out(summed[a][:, :, c - a : d - a], c, d)
 
-        fetch_add(FIRST, ((0, 1), (1, 2), (2, 3), (3, 4)))
+        for a, b in (FIRST, SECOND, SHARED, LAST):
+            summed[a] = keep.tile([P, PACK, b - a], F32, name="summed_%d" % a)
+        for t in range(PACK):
+            fetch_add(FIRST, t)
+            store_out(FIRST, t, t + 1)
+            if t == 1:
+                load_res(LAST, 0, PACK, "res_0_0")
         round_range(FIRST, 0, 512)
-        round_range(FIRST, 512, 768)
-        fetch_add(SECOND, ((0, 2), (2, 4)))
-        round_range(SECOND, *SECOND)
+        round_range(FIRST, 512, 832)
+        fetch_add(SECOND, 0)
         a, b = SHARED
-        summed[a] = keep.tile([P, PACK, b - a], F32, name="summed_%d" % a)
         for u in range(2):
             nc.vector.tensor_tensor(summed[a][:, 2 * u : 2 * u + 2, :], fetched[u][:], residual(2 * u, 2 * u + 2, a), ADD)
             store_out(SHARED, 2 * u, 2 * u + 2)
-        round_range(SHARED, 1152, 1536)
-        round_range(SHARED, 1536, 1792)
+        round_range(SHARED, 832, 1024)
+        round_range(SHARED, 1024, 1472)
+        fetch_add(SECOND, 1)
+        store_out(SECOND, 0, 2)
         quantize_out(0, 512)
-        quantize_out(512, 768)
-        store_words(0, 768)
-        store_scales(0, 768, [nc.sync] * 4)
-        fetch_add(LAST, ((0, 2), (2, 4)))
-        quantize_out(*SECOND)
-        store_words(*SECOND)
+        store_words(0, 512)
+        fetch_add(SECOND, 2)
+        fetch_add(SECOND, 3)
+        store_out(SECOND, 2, 4)
+        round_range(SECOND, *SECOND)
+        quantize_out(512, 1024)
+        store_scales(0, 1024, [nc.sync] * 4)
+        store_words(512, 1024)
+        for t in range(PACK):
+            fetch_add(LAST, t)
+        store_out(LAST, 0, PACK)
         round_range(LAST, *LAST)
-        quantize_out(1152, 1536)
-        quantize_out(1536, 1792)
-        store_words(*SHARED)
+        quantize_out(1024, 1408)
+        store_words(1024, 1408)
+        quantize_out(1408, 1920)
+        store_words(1408, 1920)
         quantize_out(*LAST)
         store_words(*LAST)
-        store_scales(768, U, [nc.sync] * 4)
+        store_scales(1024, U, [nc.sync] * 4)

@@ -21,11 +21,8 @@ PACK = 4
 LIST = 16
 LINE = 4
 
-X_LOADS = tuple((j, a, a + 1024) for j in range(3) for a in (0, 1024)) + ((3, 0, 1024), (3, 1024, 1536), (3, 1536, 2048))
-VECTOR_TOKENS = (0, 352)
-SCALAR_TOKENS = ((352, 608), (608, 1024))
-EARLY = 512
-FIRST_PRODUCTS = ((0, 256), (256, 512), (512, 768), (768, 896), (896, 1024))
+VECTOR_TOKENS = (320, 256)
+PRODUCTS_0 = ((0, 256), (256, 512), (512, 768), (768, 896), (896, 1024))
 FIRST, SECOND, SHARED, LAST = (0, 832), (1472, 1920), (832, 1472), (1920, 2048)
 
 
@@ -51,9 +48,9 @@ def tile_picked_unmerge_relu_lo_kernel(tc, xT, w1, res, offs, own, out_0, out_1,
         nc.scalar.activation(warm[:, 8:9], warm[:, 0:1], RELU)
 
         x_raw = [keep.tile([P, T], F32, name="x_raw_%d" % j) for j in range(PACK)]
-        for j, a, b in X_LOADS:
-            nc.sync.dma_start(x_raw[j][:, a:b], x_rows[:, j, a:b])
-            if (j, a) == (0, 0):
+        for j in range(PACK):
+            nc.sync.dma_start(x_raw[j][:], x_rows[:, j, :])
+            if j == 0:
                 nc.sync.dma_start(offs_sb[:], offs)
         w_raw = keep.tile([P, PACK, N], F32, name="w_raw")
         nc.sync.dma_start(w_raw[:], w_rows)
@@ -67,69 +64,71 @@ def tile_picked_unmerge_relu_lo_kernel(tc, xT, w1, res, offs, own, out_0, out_1,
             for t in range(t0, t1):
                 res_raw[a, t] = (part, t - t0)
 
-        for chunk, t0, t1 in ((FIRST, 0, 2), (FIRST, 2, 4), (SECOND, 0, 1), (SHARED, 0, 4), (SECOND, 1, 4)):
+        for chunk, t0, t1 in ((FIRST, 0, 1), (FIRST, 1, 2), (FIRST, 2, 3), (FIRST, 3, 4), (SECOND, 0, 1), (SHARED, 0, 4), (SECOND, 1, 4)):
             load_res(chunk, t0, t1, "res_%d_%d" % (chunk[0], t0))
 
         def residual(t0, t1, a):
             part, t = res_raw[a, t0]
             return part[:, t : t + t1 - t0, :]
 
-        x_half = [keep.tile([P, T], BF16, name="x_half_%d" % j) for j in range(PACK)]
         picked = keep.tile([P, S * PACK], BF16, name="picked", align_bytes=64)
+        picked_words = picked[:].rearrange("p (s j) -> p s j", j=PACK)
+        x_codes = keep.tile([P, S], U32, name="x_codes", align_bytes=64)
+        x_scales = keep.tile([P, S], U8, name="x_scales", align_bytes=64)
 
-        def picked_plane(j, a, b):
-            return picked[:].rearrange("p (s j) -> p s j", j=PACK)[:, a:b, j]
+        def quantize_x(a, b):
+            nc.vector.quantize_mx(out=x_codes[:, a:b].bitcast(FP8X4), scales=x_scales[:, a:b], in_=picked[:, a * PACK : b * PACK])
 
-        for j in range(PACK):
-            for i, a, b in X_LOADS:
-                if i == j:
-                    nc.vector.tensor_copy(x_half[j][:, a:b], x_raw[j][:, a:b])
-            a, b = VECTOR_TOKENS
-            nc.vector.tensor_copy(picked_plane(j, a, b), x_raw[j][:].indirect(offs_sb[:, a // LIST : b // LIST]))
-            for a, b in SCALAR_TOKENS:
-                nc.scalar.activation(picked_plane(j, a, b), x_half[j][:].indirect(offs_sb[:, a // LIST : b // LIST]), COPY)
+        flat = {}
+
+        def gather_pair(u, pieces):
+            first = VECTOR_TOKENS[u]
+            for a, b in pieces:
+                flat[u, a] = keep.tile([P, 2, b - a], BF16, name="flat_%d_%d" % (u, a))
+            for e in range(2):
+                window = x_raw[2 * u + e]
+                nc.vector.tensor_copy(picked_words[:, 0:first, 2 * u + e], window[:].indirect(offs_sb[:, 0 : first // LIST]))
+                for a, b in pieces:
+                    nc.scalar.activation(flat[u, a][:, e, :], window[:].indirect(offs_sb[:, a // LIST : b // LIST]), COPY)
+
+        def weave(u, a, b):
+            nc.vector.tensor_copy(picked_words[:, a:b, 2 * u : 2 * u + 2], flat[u, a][:].rearrange("p e s -> p s e"))
+
+        gather_pair(0, ((320, S),))
+        weave(0, 320, S)
+        gather_pair(1, ((256, 512), (512, 768), (768, S)))
+        weave(1, 256, 512)
+        quantize_x(0, 256)
+        weave(1, 512, 768)
+        quantize_x(256, 512)
+        weave(1, 768, S)
+        quantize_x(512, 768)
+        quantize_x(768, S)
 
         w_dealt = [keep.tile([P, 2 * P * PACK], BF16, name="w_dealt_%d" % u, tag="w_dealt_%d" % u, align_bytes=64) for u in range(2)]
         w_codes = keep.tile([P, N], U32, name="w_codes", align_bytes=64)
         w_scales = keep.tile([P, N], U8, name="w_scales", align_bytes=64)
 
-        def deal(copy, u):
-            src = w_raw[:].rearrange("p j (m t) -> p m j t", t=PACK)[:, :, :, 2 * u : 2 * u + 2]
-            copy(w_dealt[u][:].rearrange("p (t m j) -> p m j t", t=2, j=PACK), src)
+        def deal(copy, u, m0, m1):
+            src = w_raw[:].rearrange("p j (m t) -> p m j t", t=PACK)[:, m0:m1, :, 2 * u : 2 * u + 2]
+            copy(w_dealt[u][:].rearrange("p (t m j) -> p m j t", t=2, j=PACK)[:, m0:m1], src)
 
         def quantize_w(t0, t1):
             src = w_dealt[t0 // 2][:, t0 % 2 * P * PACK : (t0 % 2 + t1 - t0) * P * PACK]
             nc.vector.quantize_mx(out=w_codes[:, t0 * P : t1 * P].bitcast(FP8X4), scales=w_scales[:, t0 * P : t1 * P], in_=src)
 
-        x_codes = [keep.tile([P, EARLY], U32, name="x_low", align_bytes=64)]
-        x_scales = [keep.tile([P, n], U8, name="x_scales_%d" % a, align_bytes=64) for a, n in ((0, EARLY), (EARLY, S - EARLY))]
-
-        def quantize_x(a, b):
-            first = a // EARLY * EARLY
-            cols = slice(a - first, b - first)
-            src = picked[:, a * PACK : b * PACK]
-            nc.vector.quantize_mx(out=x_codes[a // EARLY][:, cols].bitcast(FP8X4), scales=x_scales[a // EARLY][:, cols], in_=src)
-
-        for a, b in FIRST_PRODUCTS[:2]:
-            quantize_x(a, b)
-        deal(nc.vector.tensor_copy, 0)
-        deal(nc.scalar.copy, 1)
+        deal(nc.scalar.copy, 0, 0, P)
+        deal(nc.scalar.copy, 1, 0, P)
         quantize_w(0, 1)
         quantize_w(1, 2)
-        x_codes.append(keep.tile([P, S - EARLY], U32, name="x_high", tag="w_dealt_0", align_bytes=64))
-        for a, b in FIRST_PRODUCTS[2:]:
-            quantize_x(a, b)
-        quantize_w(2, 4)
 
         def product(out, t, a, b):
-            first = a // EARLY * EARLY
-            cols = slice(a - first, b - first)
             nc.tensor.matmul_mx(
                 out=out,
                 lhsT=w_codes[:, t * P : (t + 1) * P].bitcast(FP8X4),
                 lhsT_scale=w_scales[:, t * P : (t + 1) * P],
-                rhs=x_codes[a // EARLY][:, cols].bitcast(FP8X4),
-                rhs_scale=x_scales[a // EARLY][:, cols],
+                rhs=x_codes[:, a:b].bitcast(FP8X4),
+                rhs_scale=x_scales[:, a:b],
                 start=True,
                 stop=True,
             )
@@ -137,13 +136,16 @@ def tile_picked_unmerge_relu_lo_kernel(tc, xT, w1, res, offs, own, out_0, out_1,
         y = []
         for t in range(PACK):
             y.append(keep.tile([P, S], F32, name="y_%d" % t))
-            for a, b in FIRST_PRODUCTS if t == 0 else ((0, 512), (512, 1024)):
+            for a, b in PRODUCTS_0 if t == 0 else ((0, 512), (512, 1024)):
                 acc = psum.tile([P, 512], F32, name="acc")
                 product(acc[:, 0 : b - a], t, a, b)
-                if (t, a) == (0, 512):
+                if t == 0 and a in (0, 256, 896):
                     nc.vector.tensor_scalar_max(y[t][:, a:b], acc[:, 0 : b - a], 0.0)
                 else:
                     nc.scalar.activation(y[t][:, a:b], acc[:, 0 : b - a], RELU)
+
+            if t == 0:
+                quantize_w(2, 4)
 
         scales = keep.tile([P, U], U8, name="scales", align_bytes=64)
 
@@ -190,18 +192,20 @@ def tile_picked_unmerge_relu_lo_kernel(tc, xT, w1, res, offs, own, out_0, out_1,
             fetch_add(FIRST, t)
             store_out(FIRST, t, t + 1)
             if t == 1:
-                load_res(LAST, 0, PACK, "res_0_0")
+                load_res(LAST, 0, PACK, "res_0_1")
         round_range(FIRST, 0, 512)
         round_range(FIRST, 512, 832)
         fetch_add(SECOND, 0)
+        store_out(SECOND, 0, 1)
         a, b = SHARED
         for u in range(2):
             nc.vector.tensor_tensor(summed[a][:, 2 * u : 2 * u + 2, :], fetched[u][:], residual(2 * u, 2 * u + 2, a), ADD)
-            store_out(SHARED, 2 * u, 2 * u + 2)
+            store_out(SHARED, 2 * u, 2 * u + 1)
+            store_out(SHARED, 2 * u + 1, 2 * u + 2)
         round_range(SHARED, 832, 1024)
         round_range(SHARED, 1024, 1472)
         fetch_add(SECOND, 1)
-        store_out(SECOND, 0, 2)
+        store_out(SECOND, 1, 2)
         quantize_out(0, 512)
         store_words(0, 512)
         fetch_add(SECOND, 2)

@@ -73,11 +73,17 @@ def tile_picked_unmerge_relu_lo_kernel(tc, xT, w1, res, offs, own, out_0, out_1,
 
         picked = keep.tile([P, S * PACK], BF16, name="picked", align_bytes=64)
         picked_words = picked[:].rearrange("p (s j) -> p s j", j=PACK)
-        x_codes = keep.tile([P, S], U32, name="x_codes", align_bytes=64)
+        early_codes = keep.tile([P, S // 2], U32, name="early_codes", align_bytes=64)
+        x_codes = {0: early_codes}
+
+        def codes(a, b):
+            base = a // 512 * 512
+            return x_codes[base][:, a - base : b - base].bitcast(FP8X4)
+
         x_scales = keep.tile([P, S], U8, name="x_scales", align_bytes=64)
 
         def quantize_x(a, b):
-            nc.vector.quantize_mx(out=x_codes[:, a:b].bitcast(FP8X4), scales=x_scales[:, a:b], in_=picked[:, a * PACK : b * PACK])
+            nc.vector.quantize_mx(out=codes(a, b), scales=x_scales[:, a:b], in_=picked[:, a * PACK : b * PACK])
 
         flat = {}
 
@@ -91,8 +97,8 @@ def tile_picked_unmerge_relu_lo_kernel(tc, xT, w1, res, offs, own, out_0, out_1,
                 for a, b in pieces:
                     nc.scalar.activation(flat[u, a][:, e, :], window[:].indirect(offs_sb[:, a // LIST : b // LIST]), COPY)
 
-        def weave(u, a, b):
-            nc.vector.tensor_copy(picked_words[:, a:b, 2 * u : 2 * u + 2], flat[u, a][:].rearrange("p e s -> p s e"))
+        def weave(u, a, b, copy=nc.vector.tensor_copy):
+            copy(picked_words[:, a:b, 2 * u : 2 * u + 2], flat[u, a][:].rearrange("p e s -> p s e"))
 
         gather_pair(0, ((320, S),))
         weave(0, 320, S)
@@ -101,33 +107,37 @@ def tile_picked_unmerge_relu_lo_kernel(tc, xT, w1, res, offs, own, out_0, out_1,
         quantize_x(0, 256)
         weave(1, 512, 768)
         quantize_x(256, 512)
-        weave(1, 768, S)
-        quantize_x(512, 768)
-        quantize_x(768, S)
+        weave(1, 768, S, nc.scalar.copy)
 
-        w_dealt = [keep.tile([P, 2 * P * PACK], BF16, name="w_dealt_%d" % u, tag="w_dealt_%d" % u, align_bytes=64) for u in range(2)]
+        w_dealt = {}
         w_codes = keep.tile([P, N], U32, name="w_codes", align_bytes=64)
         w_scales = keep.tile([P, N], U8, name="w_scales", align_bytes=64)
 
         def deal(copy, u, m0, m1):
+            w_dealt[u, m0] = keep.tile([P, 2, (m1 - m0) * PACK], BF16, name="w_dealt_%d_%d" % (u, m0), tag="w_dealt_%d_%d" % (u, m0), align_bytes=64)
             src = w_raw[:].rearrange("p j (m t) -> p m j t", t=PACK)[:, m0:m1, :, 2 * u : 2 * u + 2]
-            copy(w_dealt[u][:].rearrange("p (t m j) -> p m j t", t=2, j=PACK)[:, m0:m1], src)
+            copy(w_dealt[u, m0][:].rearrange("p t (m j) -> p m j t", j=PACK), src)
 
-        def quantize_w(t0, t1):
-            src = w_dealt[t0 // 2][:, t0 % 2 * P * PACK : (t0 % 2 + t1 - t0) * P * PACK]
-            nc.vector.quantize_mx(out=w_codes[:, t0 * P : t1 * P].bitcast(FP8X4), scales=w_scales[:, t0 * P : t1 * P], in_=src)
+        def quantize_w(t, m0, m1):
+            cols = slice(t * P + m0, t * P + m1)
+            nc.vector.quantize_mx(out=w_codes[:, cols].bitcast(FP8X4), scales=w_scales[:, cols], in_=w_dealt[t // 2, m0][:, t % 2, :])
 
-        deal(nc.scalar.copy, 0, 0, P)
+        deal(nc.vector.tensor_copy, 0, 0, 64)
+        deal(nc.vector.tensor_copy, 0, 64, P)
         deal(nc.scalar.copy, 1, 0, P)
-        quantize_w(0, 1)
-        quantize_w(1, 2)
+        for t in range(2):
+            quantize_w(t, 0, 64)
+            quantize_w(t, 64, P)
+        x_codes[512] = keep.tile([P, S // 2], U32, name="late_codes", tag="w_dealt_0_0", align_bytes=64)
+        quantize_x(512, 768)
+        quantize_x(768, S)
 
         def product(out, t, a, b):
             nc.tensor.matmul_mx(
                 out=out,
                 lhsT=w_codes[:, t * P : (t + 1) * P].bitcast(FP8X4),
                 lhsT_scale=w_scales[:, t * P : (t + 1) * P],
-                rhs=x_codes[:, a:b].bitcast(FP8X4),
+                rhs=codes(a, b),
                 rhs_scale=x_scales[:, a:b],
                 start=True,
                 stop=True,
@@ -139,13 +149,15 @@ def tile_picked_unmerge_relu_lo_kernel(tc, xT, w1, res, offs, own, out_0, out_1,
             for a, b in PRODUCTS_0 if t == 0 else ((0, 512), (512, 1024)):
                 acc = psum.tile([P, 512], F32, name="acc")
                 product(acc[:, 0 : b - a], t, a, b)
-                if t == 0 and a in (0, 256, 896):
+                if t == 0 and a in (256, 512):
                     nc.vector.tensor_scalar_max(y[t][:, a:b], acc[:, 0 : b - a], 0.0)
                 else:
                     nc.scalar.activation(y[t][:, a:b], acc[:, 0 : b - a], RELU)
 
             if t == 0:
-                quantize_w(2, 4)
+                nc.vector.quantize_mx(
+                    out=w_codes[:, 2 * P :].bitcast(FP8X4), scales=w_scales[:, 2 * P :], in_=w_dealt[1, 0][:].rearrange("p t c -> p (t c)")
+                )
 
         scales = keep.tile([P, U], U8, name="scales", align_bytes=64)
 

@@ -23,7 +23,7 @@ LINE = 4
 
 VECTOR_TOKENS = (320, 256)
 PRODUCTS_0 = ((0, 256), (256, 512), (512, 768), (768, 896), (896, 1024))
-FIRST, SECOND, SHARED, LAST = (0, 832), (1472, 1920), (832, 1472), (1920, 2048)
+FIRST, SECOND, SHARED, LAST = (0, 928), (1568, 1920), (928, 1568), (1920, 2048)
 
 
 def tile_picked_unmerge_relu_lo_kernel(tc, xT, w1, res, offs, own, out_0, out_1, out_2):
@@ -159,7 +159,12 @@ def tile_picked_unmerge_relu_lo_kernel(tc, xT, w1, res, offs, own, out_0, out_1,
                     out=w_codes[:, 2 * P :].bitcast(FP8X4), scales=w_scales[:, 2 * P :], in_=w_dealt[1, 0][:].rearrange("p t c -> p (t c)")
                 )
 
-        scales = keep.tile([P, U], U8, name="scales", align_bytes=64)
+        scale_halves = [keep.tile([P, U // 2], U8, name="scales_%d" % h, align_bytes=64) for h in range(2)]
+
+        def scales(a, b):
+            h = a // (U // 2)
+            return scale_halves[h][:, a - h * U // 2 : b - h * U // 2]
+
 
         a, b = SHARED
         fetched = [keep.tile([P, 2, b - a], F32, name="fetched_%d" % u, tag="fetched_%d" % u) for u in range(2)]
@@ -173,13 +178,13 @@ def tile_picked_unmerge_relu_lo_kernel(tc, xT, w1, res, offs, own, out_0, out_1,
             nc.scalar.copy(rounded[:, a * PACK : b * PACK].rearrange("p (c i t) -> p c t i", i=LINE, t=PACK), src)
 
         def store_scales(a, b, queues):
-            for q in range(4):
-                queues[q].dma_start(out_scales[4 * q : 4 * q + 4, a // 4 : b // 4], scales[32 * q : 32 * q + 4, a:b].bitcast(I32))
+            for r in range(4):
+                queues[r].dma_start(out_scales[r:16:4, a // 4 : b // 4], scale_halves[a // (U // 2)][r:P:32, :].bitcast(I32))
 
         words = keep.tile([P, U], U32, name="words", align_bytes=64)
 
         def quantize_out(a, b):
-            nc.vector.quantize_mx(out=words[:, a:b].bitcast(FP8X4), scales=scales[:, a:b], in_=rounded[:, a * PACK : b * PACK])
+            nc.vector.quantize_mx(out=words[:, a:b].bitcast(FP8X4), scales=scales(a, b), in_=rounded[:, a * PACK : b * PACK])
 
         def store_words(a, b):
             nc.sync.dma_start(out_words[:, a:b], words[:, a:b].bitcast(I32))
@@ -206,7 +211,7 @@ def tile_picked_unmerge_relu_lo_kernel(tc, xT, w1, res, offs, own, out_0, out_1,
             if t == 1:
                 load_res(LAST, 0, PACK, "res_0_1")
         round_range(FIRST, 0, 512)
-        round_range(FIRST, 512, 832)
+        round_range(FIRST, 512, FIRST[1])
         fetch_add(SECOND, 0)
         store_out(SECOND, 0, 1)
         a, b = SHARED
@@ -214,27 +219,27 @@ def tile_picked_unmerge_relu_lo_kernel(tc, xT, w1, res, offs, own, out_0, out_1,
             nc.vector.tensor_tensor(summed[a][:, 2 * u : 2 * u + 2, :], fetched[u][:], residual(2 * u, 2 * u + 2, a), ADD)
             store_out(SHARED, 2 * u, 2 * u + 1)
             store_out(SHARED, 2 * u + 1, 2 * u + 2)
-        round_range(SHARED, 832, 1024)
-        round_range(SHARED, 1024, 1472)
+        round_range(SHARED, SHARED[0], 1024)
+        round_range(SHARED, 1024, SHARED[1])
         fetch_add(SECOND, 1)
         store_out(SECOND, 1, 2)
         quantize_out(0, 512)
         store_words(0, 512)
         fetch_add(SECOND, 2)
+        quantize_out(512, 1024)
+        store_words(512, 1024)
+        store_scales(0, 1024, [nc.sync] * 4)
         fetch_add(SECOND, 3)
         store_out(SECOND, 2, 4)
         round_range(SECOND, *SECOND)
-        quantize_out(512, 1024)
-        store_scales(0, 1024, [nc.sync] * 4)
-        store_words(512, 1024)
         for t in range(PACK):
             fetch_add(LAST, t)
         store_out(LAST, 0, PACK)
         round_range(LAST, *LAST)
-        quantize_out(1024, 1408)
-        store_words(1024, 1408)
-        quantize_out(1408, 1920)
-        store_words(1408, 1920)
+        quantize_out(1024, 1536)
+        store_words(1024, 1536)
+        quantize_out(1536, 1920)
+        store_words(1536, 1920)
         quantize_out(*LAST)
         store_words(*LAST)
         store_scales(1024, U, [nc.sync] * 4)

@@ -19,7 +19,7 @@ ADD = mybir.AluOpType.add
 P = 128
 PACK = 4
 LIST = 16
-LINE = 4
+LINE = 2
 
 VECTOR_TOKENS = (320, 256)
 PRODUCTS_0 = ((0, 256), (256, 512), (512, 768), (768, 896), (896, 1024))

@@ -23,7 +23,7 @@ LINE = 2
 
 VECTOR_TOKENS = (320, 256)
 PRODUCTS_0 = ((0, 256), (256, 512), (512, 768), (768, 896), (896, 1024))
-FIRST, SECOND, SHARED, LAST = (0, 928), (1568, 1920), (928, 1568), (1920, 2048)
+FIRST, SECOND, SHARED, LAST = (0, 896), (1600, 1920), (896, 1600), (1920, 2048)
 
 
 def tile_picked_unmerge_relu_lo_kernel(tc, xT, w1, res, offs, own, out_0, out_1, out_2):

@@ -1,3 +1,4 @@
+import math
 from contextlib import ExitStack
 
 import concourse.mybir as mybir
@@ -23,6 +24,8 @@ LINE = 2
 
 VECTOR_TOKENS = (320, 256)
 PRODUCTS_0 = ((0, 256), (256, 512), (512, 768), (768, 896), (896, 1024))
+KIB = 1024
+PLACES = {"res": 0, "warm": 30, "x_0": 32, "picked": 40, "y": 70.25, "flat": 86.25, "summed": 99.25, "w": 132, "x_1": 148, "fetched": 160.25, "words": 177.25, "x_2": 187.25, "rounded": 195.25, "x_3": 212}
 FIRST, SECOND, SHARED, LAST = (0, 896), (1600, 1920), (896, 1600), (1920, 2048)
 
 
@@ -40,26 +43,37 @@ def tile_picked_unmerge_relu_lo_kernel(tc, xT, w1, res, offs, own, out_0, out_1,
         keep = ctx.enter_context(tc.tile_pool(name="keep", bufs=1))
         psum = ctx.enter_context(tc.psum_pool(name="psum", bufs=8))
 
+        taken = {group: int(start * KIB) for group, start in PLACES.items()}
+        tag_places = {}
+
+        def place(group, shape, dtype, size, name, tag=None, room=0):
+            tag = tag or name
+            if tag not in tag_places:
+                tag_places[tag] = taken[group]
+                taken[group] = taken[group] + max(room, size * math.prod(shape[1:]))
+            return keep.tile(shape, dtype, name=name, tag=tag, align_bytes=256, offset=tag_places[tag])
+
         offs_sb = lists.tile([P, S // LIST], U16, name="offs_sb")
         own_sb = lists.tile([P, U // LIST], U16, name="own_sb")
 
-        warm = keep.tile([P, 16], F32, name="warm")
+        warm = keep.tile([P, 16], F32, name="warm", align_bytes=16 * KIB, offset=64 * KIB)
         nc.vector.memset(warm[:, 0:1], 0.0)
         nc.scalar.activation(warm[:, 8:9], warm[:, 0:1], RELU)
 
-        x_raw = [keep.tile([P, T], F32, name="x_raw_%d" % j) for j in range(PACK)]
+        x_raw = [place("x_%d" % j, [P, T], F32, 4, "x_raw_%d" % j) for j in range(PACK)]
         for j in range(PACK):
             nc.sync.dma_start(x_raw[j][:], x_rows[:, j, :])
             if j == 0:
                 nc.sync.dma_start(offs_sb[:], offs)
-        w_raw = keep.tile([P, PACK, N], F32, name="w_raw")
+        w_raw = keep.tile([P, PACK, N], F32, name="w_raw", align_bytes=256, offset=taken["w"])
+        taken["w"] = taken["w"] + 8 * KIB
         nc.sync.dma_start(w_raw[:], w_rows)
         nc.sync.dma_start(own_sb[:], own)
         res_raw = {}
 
         def load_res(chunk, t0, t1, tag):
             a, b = chunk
-            part = keep.tile([P, t1 - t0, b - a], F32, name="res_%d_%d" % (a, t0), tag=tag)
+            part = place("res", [P, t1 - t0, b - a], F32, 4, "res_%d_%d" % (a, t0), tag)
             nc.sync.dma_start(part[:], res_rows[:, t0:t1, a:b])
             for t in range(t0, t1):
                 res_raw[a, t] = (part, t - t0)
@@ -71,16 +85,16 @@ def tile_picked_unmerge_relu_lo_kernel(tc, xT, w1, res, offs, own, out_0, out_1,
             part, t = res_raw[a, t0]
             return part[:, t : t + t1 - t0, :]
 
-        picked = keep.tile([P, S * PACK], BF16, name="picked", align_bytes=64)
+        picked = place("picked", [P, S * PACK], BF16, 2, "picked")
         picked_words = picked[:].rearrange("p (s j) -> p s j", j=PACK)
-        early_codes = keep.tile([P, S // 2], U32, name="early_codes", align_bytes=64)
+        early_codes = place("w", [P, S // 2], U32, 4, "early_codes")
         x_codes = {0: early_codes}
 
         def codes(a, b):
             base = a // 512 * 512
             return x_codes[base][:, a - base : b - base].bitcast(FP8X4)
 
-        x_scales = keep.tile([P, S], U8, name="x_scales", align_bytes=64)
+        x_scales = place("w", [P, S], U8, 1, "x_scales")
 
         def quantize_x(a, b):
             nc.vector.quantize_mx(out=codes(a, b), scales=x_scales[:, a:b], in_=picked[:, a * PACK : b * PACK])
@@ -90,7 +104,7 @@ def tile_picked_unmerge_relu_lo_kernel(tc, xT, w1, res, offs, own, out_0, out_1,
         def gather_pair(u, pieces):
             first = VECTOR_TOKENS[u]
             for a, b in pieces:
-                flat[u, a] = keep.tile([P, 2, b - a], BF16, name="flat_%d_%d" % (u, a))
+                flat[u, a] = place("flat", [P, 2, b - a], BF16, 2, "flat_%d_%d" % (u, a))
             for e in range(2):
                 window = x_raw[2 * u + e]
                 nc.vector.tensor_copy(picked_words[:, 0:first, 2 * u + e], window[:].indirect(offs_sb[:, 0 : first // LIST]))
@@ -110,11 +124,11 @@ def tile_picked_unmerge_relu_lo_kernel(tc, xT, w1, res, offs, own, out_0, out_1,
         weave(1, 768, S, nc.scalar.copy)
 
         w_dealt = {}
-        w_codes = keep.tile([P, N], U32, name="w_codes", align_bytes=64)
-        w_scales = keep.tile([P, N], U8, name="w_scales", align_bytes=64)
+        w_codes = place("w", [P, N], U32, 4, "w_codes")
+        w_scales = place("w", [P, N], U8, 1, "w_scales")
 
         def deal(copy, u, m0, m1):
-            w_dealt[u, m0] = keep.tile([P, 2, (m1 - m0) * PACK], BF16, name="w_dealt_%d_%d" % (u, m0), tag="w_dealt_%d_%d" % (u, m0), align_bytes=64)
+            w_dealt[u, m0] = place("picked", [P, 2, (m1 - m0) * PACK], BF16, 2, "w_dealt_%d_%d" % (u, m0), room=2 * KIB)
             src = w_raw[:].rearrange("p j (m t) -> p m j t", t=PACK)[:, m0:m1, :, 2 * u : 2 * u + 2]
             copy(w_dealt[u, m0][:].rearrange("p t (m j) -> p m j t", j=PACK), src)
 
@@ -128,7 +142,7 @@ def tile_picked_unmerge_relu_lo_kernel(tc, xT, w1, res, offs, own, out_0, out_1,
         for t in range(2):
             quantize_w(t, 0, 64)
             quantize_w(t, 64, P)
-        x_codes[512] = keep.tile([P, S // 2], U32, name="late_codes", tag="w_dealt_0_0", align_bytes=64)
+        x_codes[512] = place("picked", [P, S // 2], U32, 4, "late_codes", "w_dealt_0_0")
         quantize_x(512, 768)
         quantize_x(768, S)
 
@@ -145,7 +159,7 @@ def tile_picked_unmerge_relu_lo_kernel(tc, xT, w1, res, offs, own, out_0, out_1,
 
         y = []
         for t in range(PACK):
-            y.append(keep.tile([P, S], F32, name="y_%d" % t))
+            y.append(place("y", [P, S], F32, 4, "y_%d" % t))
             for a, b in PRODUCTS_0 if t == 0 else ((0, 512), (512, 1024)):
                 acc = psum.tile([P, 512], F32, name="acc")
                 product(acc[:, 0 : b - a], t, a, b)
@@ -159,7 +173,7 @@ def tile_picked_unmerge_relu_lo_kernel(tc, xT, w1, res, offs, own, out_0, out_1,
                     out=w_codes[:, 2 * P :].bitcast(FP8X4), scales=w_scales[:, 2 * P :], in_=w_dealt[1, 0][:].rearrange("p t c -> p (t c)")
                 )
 
-        scale_halves = [keep.tile([P, U // 2], U8, name="scales_%d" % h, align_bytes=64) for h in range(2)]
+        scale_halves = [place("words", [P, U // 2], U8, 1, "scales_%d" % h) for h in range(2)]
 
         def scales(a, b):
             h = a // (U // 2)
@@ -167,11 +181,11 @@ def tile_picked_unmerge_relu_lo_kernel(tc, xT, w1, res, offs, own, out_0, out_1,
 
 
         a, b = SHARED
-        fetched = [keep.tile([P, 2, b - a], F32, name="fetched_%d" % u, tag="fetched_%d" % u) for u in range(2)]
+        fetched = [place("fetched", [P, 2, b - a], F32, 4, "fetched_%d" % u) for u in range(2)]
         for t in range(PACK):
             nc.scalar.activation(fetched[t // 2][:, t % 2, :], y[t][:].indirect(own_sb[:, a // LIST : b // LIST]), COPY)
 
-        rounded = keep.tile([P, U * PACK], BF16, name="rounded", align_bytes=64)
+        rounded = place("rounded", [P, U * PACK], BF16, 2, "rounded")
 
         def round_out(summed, a, b):
             src = summed.rearrange("p t (c i) -> p c t i", i=LINE)
@@ -181,7 +195,7 @@ def tile_picked_unmerge_relu_lo_kernel(tc, xT, w1, res, offs, own, out_0, out_1,
             for r in range(4):
                 queues[r].dma_start(out_scales[r:16:4, a // 4 : b // 4], scale_halves[a // (U // 2)][r:P:32, :].bitcast(I32))
 
-        words = keep.tile([P, U], U32, name="words", align_bytes=64)
+        words = place("words", [P, U], U32, 4, "words")
 
         def quantize_out(a, b):
             nc.vector.quantize_mx(out=words[:, a:b].bitcast(FP8X4), scales=scales(a, b), in_=rounded[:, a * PACK : b * PACK])
@@ -204,7 +218,7 @@ def tile_picked_unmerge_relu_lo_kernel(tc, xT, w1, res, offs, own, out_0, out_1,
             round_out(summed[a][:, :, c - a : d - a], c, d)
 
         for a, b in (FIRST, SECOND, SHARED, LAST):
-            summed[a] = keep.tile([P, PACK, b - a], F32, name="summed_%d" % a)
+            summed[a] = place("summed", [P, PACK, b - a], F32, 4, "summed_%d" % a)
         for t in range(PACK):
             fetch_add(FIRST, t)
             store_out(FIRST, t, t + 1)

@@ -25,7 +25,7 @@ LINE = 2
 VECTOR_TOKENS = (320, 256)
 PRODUCTS_0 = ((0, 256), (256, 512), (512, 768), (768, 896), (896, 1024))
 KIB = 1024
-PLACES = {"res": 0, "warm": 30, "x_0": 32, "picked": 40, "y": 70.25, "flat": 86.25, "summed": 99.25, "w": 132, "x_1": 148, "fetched": 160.25, "words": 177.25, "x_2": 187.25, "rounded": 195.25, "x_3": 212}
+PLACES = {"res": 24, "x_0": 0, "picked": 38, "dealt": 50.25, "y": 70.25, "flat": 32.25, "summed": 99.25, "w": 132, "x_1": 148, "fetched": 160.25, "words": 177.25, "x_2": 24, "rounded": 195.25, "x_3": 212}
 FIRST, SECOND, SHARED, LAST = (0, 896), (1600, 1920), (896, 1600), (1920, 2048)
 
 
@@ -78,8 +78,6 @@ def tile_picked_unmerge_relu_lo_kernel(tc, xT, w1, res, offs, own, out_0, out_1,
             for t in range(t0, t1):
                 res_raw[a, t] = (part, t - t0)
 
-        for chunk, t0, t1 in ((FIRST, 0, 1), (FIRST, 1, 2), (FIRST, 2, 3), (FIRST, 3, 4), (SECOND, 0, 1), (SHARED, 0, 4), (SECOND, 1, 4)):
-            load_res(chunk, t0, t1, "res_%d_%d" % (chunk[0], t0))
 
         def residual(t0, t1, a):
             part, t = res_raw[a, t0]
@@ -128,7 +126,7 @@ def tile_picked_unmerge_relu_lo_kernel(tc, xT, w1, res, offs, own, out_0, out_1,
         w_scales = place("w", [P, N], U8, 1, "w_scales")
 
         def deal(copy, u, m0, m1):
-            w_dealt[u, m0] = place("picked", [P, 2, (m1 - m0) * PACK], BF16, 2, "w_dealt_%d_%d" % (u, m0), room=2 * KIB)
+            w_dealt[u, m0] = place("w" if (u, m0) == (0, 0) else "dealt", [P, 2, (m1 - m0) * PACK], BF16, 2, "w_dealt_%d_%d" % (u, m0), room=2 * KIB)
             src = w_raw[:].rearrange("p j (m t) -> p m j t", t=PACK)[:, m0:m1, :, 2 * u : 2 * u + 2]
             copy(w_dealt[u, m0][:].rearrange("p t (m j) -> p m j t", j=PACK), src)
 
@@ -173,6 +171,8 @@ def tile_picked_unmerge_relu_lo_kernel(tc, xT, w1, res, offs, own, out_0, out_1,
                     out=w_codes[:, 2 * P :].bitcast(FP8X4), scales=w_scales[:, 2 * P :], in_=w_dealt[1, 0][:].rearrange("p t c -> p (t c)")
                 )
 
+        for chunk, t0, t1 in ((FIRST, 0, 1), (FIRST, 1, 2), (FIRST, 2, 3), (FIRST, 3, 4), (SECOND, 0, 1), (SHARED, 0, 4), (SECOND, 1, 4)):
+            load_res(chunk, t0, t1, "res_%d_%d" % (chunk[0], t0))
         scale_halves = [place("words", [P, U // 2], U8, 1, "scales_%d" % h) for h in range(2)]
 
         def scales(a, b):

import math
from contextlib import ExitStack

import concourse.mybir as mybir

K, T, S, N, U = 512, 2048, 1024, 512, 2048
FLOPS = 2 * K * N * S

F32 = mybir.dt.float32
BF16 = mybir.dt.bfloat16
U32 = mybir.dt.uint32
I32 = mybir.dt.int32
U16 = mybir.dt.uint16
U8 = mybir.dt.uint8
FP8X4 = mybir.dt.float8_e4m3fn_x4
COPY = mybir.ActivationFunctionType.Copy
RELU = mybir.ActivationFunctionType.Relu
ADD = mybir.AluOpType.add

P = 128
PACK = 4
LIST = 16
LINE = 2

VECTOR_TOKENS = (320, 256)
PRODUCTS_0 = ((0, 256), (256, 512), (512, 768), (768, 896), (896, 1024))
KIB = 1024
PLACES = {"res": 24, "x_0": 0, "picked": 38, "dealt": 50.25, "y": 70.25, "flat": 32.25, "summed": 99.25, "w": 132, "x_1": 148, "fetched": 160.25, "words": 177.25, "x_2": 24, "rounded": 195.25, "x_3": 212}
FIRST, SECOND, SHARED, LAST = (0, 896), (1600, 1920), (896, 1600), (1920, 2048)


def tile_picked_unmerge_relu_lo_kernel(tc, xT, w1, res, offs, own, out_0, out_1, out_2):
    nc = tc.nc
    x_rows = xT.rearrange("(p j) c -> p j c", j=PACK)
    w_rows = w1.rearrange("(p j) c -> p j c", j=PACK)
    res_rows = res.rearrange("(p j) c -> p j c", j=PACK)
    out_rows = out_0.rearrange("(p j) c -> p j c", j=PACK)
    out_words = out_1[0].rearrange("p c r -> p (c r)").bitcast(I32)
    out_scales = out_2[0].bitcast(I32)

    with ExitStack() as ctx:
        lists = ctx.enter_context(tc.tile_pool(name="lists", bufs=1))
        keep = ctx.enter_context(tc.tile_pool(name="keep", bufs=1))
        psum = ctx.enter_context(tc.psum_pool(name="psum", bufs=8))

        taken = {group: int(start * KIB) for group, start in PLACES.items()}
        tag_places = {}

        def place(group, shape, dtype, size, name, tag=None, room=0):
            tag = tag or name
            if tag not in tag_places:
                tag_places[tag] = taken[group]
                taken[group] = taken[group] + max(room, size * math.prod(shape[1:]))
            return keep.tile(shape, dtype, name=name, tag=tag, align_bytes=256, offset=tag_places[tag])

        offs_sb = lists.tile([P, S // LIST], U16, name="offs_sb")
        own_sb = lists.tile([P, U // LIST], U16, name="own_sb")

        warm = keep.tile([P, 16], F32, name="warm", align_bytes=16 * KIB, offset=64 * KIB)
        nc.vector.memset(warm[:, 0:1], 0.0)
        nc.scalar.activation(warm[:, 8:9], warm[:, 0:1], RELU)

        x_raw = [place("x_%d" % j, [P, T], F32, 4, "x_raw_%d" % j) for j in range(PACK)]
        for j in range(PACK):
            nc.sync.dma_start(x_raw[j][:], x_rows[:, j, :])
            if j == 0:
                nc.sync.dma_start(offs_sb[:], offs)
        w_raw = keep.tile([P, PACK, N], F32, name="w_raw", align_bytes=256, offset=taken["w"])
        taken["w"] = taken["w"] + 8 * KIB
        nc.sync.dma_start(w_raw[:], w_rows)
        nc.sync.dma_start(own_sb[:], own)
        res_raw = {}

        def load_res(chunk, t0, t1, tag):
            a, b = chunk
            part = place("res", [P, t1 - t0, b - a], F32, 4, "res_%d_%d" % (a, t0), tag)
            nc.sync.dma_start(part[:], res_rows[:, t0:t1, a:b])
            for t in range(t0, t1):
                res_raw[a, t] = (part, t - t0)


        def residual(t0, t1, a):
            part, t = res_raw[a, t0]
            return part[:, t : t + t1 - t0, :]

        picked = place("picked", [P, S * PACK], BF16, 2, "picked")
        picked_words = picked[:].rearrange("p (s j) -> p s j", j=PACK)
        early_codes = place("w", [P, S // 2], U32, 4, "early_codes")
        x_codes = {0: early_codes}

        def codes(a, b):
            base = a // 512 * 512
            return x_codes[base][:, a - base : b - base].bitcast(FP8X4)

        x_scales = place("w", [P, S], U8, 1, "x_scales")

        def quantize_x(a, b):
            nc.vector.quantize_mx(out=codes(a, b), scales=x_scales[:, a:b], in_=picked[:, a * PACK : b * PACK])

        flat = {}

        def gather_pair(u, pieces):
            first = VECTOR_TOKENS[u]
            for a, b in pieces:
                flat[u, a] = place("flat", [P, 2, b - a], BF16, 2, "flat_%d_%d" % (u, a))
            for e in range(2):
                window = x_raw[2 * u + e]
                nc.vector.tensor_copy(picked_words[:, 0:first, 2 * u + e], window[:].indirect(offs_sb[:, 0 : first // LIST]))
                for a, b in pieces:
                    nc.scalar.activation(flat[u, a][:, e, :], window[:].indirect(offs_sb[:, a // LIST : b // LIST]), COPY)

        def weave(u, a, b, copy=nc.vector.tensor_copy):
            copy(picked_words[:, a:b, 2 * u : 2 * u + 2], flat[u, a][:].rearrange("p e s -> p s e"))

        gather_pair(0, ((320, S),))
        weave(0, 320, S)
        gather_pair(1, ((256, 512), (512, 768), (768, S)))
        weave(1, 256, 512)
        quantize_x(0, 256)
        weave(1, 512, 768)
        quantize_x(256, 512)
        weave(1, 768, S, nc.scalar.copy)

        w_dealt = {}
        w_codes = place("w", [P, N], U32, 4, "w_codes")
        w_scales = place("w", [P, N], U8, 1, "w_scales")

        def deal(copy, u, m0, m1):
            w_dealt[u, m0] = place("w" if (u, m0) == (0, 0) else "dealt", [P, 2, (m1 - m0) * PACK], BF16, 2, "w_dealt_%d_%d" % (u, m0), room=2 * KIB)
            src = w_raw[:].rearrange("p j (m t) -> p m j t", t=PACK)[:, m0:m1, :, 2 * u : 2 * u + 2]
            copy(w_dealt[u, m0][:].rearrange("p t (m j) -> p m j t", j=PACK), src)

        def quantize_w(t, m0, m1):
            cols = slice(t * P + m0, t * P + m1)
            nc.vector.quantize_mx(out=w_codes[:, cols].bitcast(FP8X4), scales=w_scales[:, cols], in_=w_dealt[t // 2, m0][:, t % 2, :])

        deal(nc.vector.tensor_copy, 0, 0, 64)
        deal(nc.vector.tensor_copy, 0, 64, P)
        deal(nc.scalar.copy, 1, 0, P)
        for t in range(2):
            quantize_w(t, 0, 64)
            quantize_w(t, 64, P)
        x_codes[512] = place("picked", [P, S // 2], U32, 4, "late_codes", "w_dealt_0_0")
        quantize_x(512, 768)
        quantize_x(768, S)

        def product(out, t, a, b):
            nc.tensor.matmul_mx(
                out=out,
                lhsT=w_codes[:, t * P : (t + 1) * P].bitcast(FP8X4),
                lhsT_scale=w_scales[:, t * P : (t + 1) * P],
                rhs=codes(a, b),
                rhs_scale=x_scales[:, a:b],
                start=True,
                stop=True,
            )

        y = []
        for t in range(PACK):
            y.append(place("y", [P, S], F32, 4, "y_%d" % t))
            for a, b in PRODUCTS_0 if t == 0 else ((0, 512), (512, 1024)):
                acc = psum.tile([P, 512], F32, name="acc")
                product(acc[:, 0 : b - a], t, a, b)
                if t == 0 and a in (256, 512):
                    nc.vector.tensor_scalar_max(y[t][:, a:b], acc[:, 0 : b - a], 0.0)
                else:
                    nc.scalar.activation(y[t][:, a:b], acc[:, 0 : b - a], RELU)

            if t == 0:
                nc.vector.quantize_mx(
                    out=w_codes[:, 2 * P :].bitcast(FP8X4), scales=w_scales[:, 2 * P :], in_=w_dealt[1, 0][:].rearrange("p t c -> p (t c)")
                )

        for chunk, t0, t1 in ((FIRST, 0, 1), (FIRST, 1, 2), (FIRST, 2, 3), (FIRST, 3, 4), (SECOND, 0, 1), (SHARED, 0, 4), (SECOND, 1, 4)):
            load_res(chunk, t0, t1, "res_%d_%d" % (chunk[0], t0))
        scale_halves = [place("words", [P, U // 2], U8, 1, "scales_%d" % h) for h in range(2)]

        def scales(a, b):
            h = a // (U // 2)
            return scale_halves[h][:, a - h * U // 2 : b - h * U // 2]


        a, b = SHARED
        fetched = [place("fetched", [P, 2, b - a], F32, 4, "fetched_%d" % u) for u in range(2)]
        for t in range(PACK):
            nc.scalar.activation(fetched[t // 2][:, t % 2, :], y[t][:].indirect(own_sb[:, a // LIST : b // LIST]), COPY)

        rounded = place("rounded", [P, U * PACK], BF16, 2, "rounded")

        def round_out(summed, a, b):
            src = summed.rearrange("p t (c i) -> p c t i", i=LINE)
            nc.scalar.copy(rounded[:, a * PACK : b * PACK].rearrange("p (c i t) -> p c t i", i=LINE, t=PACK), src)

        def store_scales(a, b, queues):
            for r in range(4):
                queues[r].dma_start(out_scales[r:16:4, a // 4 : b // 4], scale_halves[a // (U // 2)][r:P:32, :].bitcast(I32))

        words = place("words", [P, U], U32, 4, "words")

        def quantize_out(a, b):
            nc.vector.quantize_mx(out=words[:, a:b].bitcast(FP8X4), scales=scales(a, b), in_=rounded[:, a * PACK : b * PACK])

        def store_words(a, b):
            nc.sync.dma_start(out_words[:, a:b], words[:, a:b].bitcast(I32))

        summed = {}

        def store_out(chunk, t0, t1):
            a, b = chunk
            nc.sync.dma_start(out_rows[:, t0:t1, a:b], summed[a][:, t0:t1, :])

        def fetch_add(chunk, t):
            a, b = chunk
            nc.vector.tensor_tensor(summed[a][:, t, :], y[t][:].indirect(own_sb[:, a // LIST : b // LIST]), residual(t, t + 1, a)[:, 0, :], ADD)

        def round_range(chunk, c, d):
            a, b = chunk
            round_out(summed[a][:, :, c - a : d - a], c, d)

        for a, b in (FIRST, SECOND, SHARED, LAST):
            summed[a] = place("summed", [P, PACK, b - a], F32, 4, "summed_%d" % a)
        for t in range(PACK):
            fetch_add(FIRST, t)
            store_out(FIRST, t, t + 1)
            if t == 1:
                load_res(LAST, 0, PACK, "res_0_1")
        round_range(FIRST, 0, 512)
        round_range(FIRST, 512, FIRST[1])
        fetch_add(SECOND, 0)
        store_out(SECOND, 0, 1)
        a, b = SHARED
        for u in range(2):
            nc.vector.tensor_tensor(summed[a][:, 2 * u : 2 * u + 2, :], fetched[u][:], residual(2 * u, 2 * u + 2, a), ADD)
            store_out(SHARED, 2 * u, 2 * u + 1)
            store_out(SHARED, 2 * u + 1, 2 * u + 2)
        round_range(SHARED, SHARED[0], 1024)
        round_range(SHARED, 1024, SHARED[1])
        fetch_add(SECOND, 1)
        store_out(SECOND, 1, 2)
        quantize_out(0, 512)
        store_words(0, 512)
        fetch_add(SECOND, 2)
        quantize_out(512, 1024)
        store_words(512, 1024)
        store_scales(0, 1024, [nc.sync] * 4)
        fetch_add(SECOND, 3)
        store_out(SECOND, 2, 4)
        round_range(SECOND, *SECOND)
        for t in range(PACK):
            fetch_add(LAST, t)
        store_out(LAST, 0, PACK)
        round_range(LAST, *LAST)
        quantize_out(1024, 1536)
        store_words(1024, 1536)
        quantize_out(1536, 1920)
        store_words(1536, 1920)
        quantize_out(*LAST)
        store_words(*LAST)
        store_scales(1024, U, [nc.sync] * 4)
